import numpy as np
import ml_dtypes


def mxq(x, axis, fmt="e4m3"):
    dtype, down = {"e4m3": (ml_dtypes.float8_e4m3fn, 7), "e5m2": (ml_dtypes.float8_e5m2, 14)}[fmt]
    v = np.moveaxis(np.asarray(x, np.float32).astype(ml_dtypes.bfloat16).astype(np.float64), axis, -1)
    blocks = v.reshape(v.shape[:-1] + (-1, 32))
    amax = np.abs(blocks).max(-1, keepdims=True)
    byte = np.maximum(np.where(amax > 0, np.frexp(amax)[1] - 1 + 127, 0) - down, 1)
    scale = np.exp2(byte - 127.0)
    codes = (blocks / scale).astype(np.float32).astype(dtype).astype(np.float64)
    return np.moveaxis((codes * scale).reshape(v.shape), -1, axis)


WIDE = False


def mx_kscale(k):
    if not WIDE:
        return np.ones(k)
    levels = np.array([10, -10, 5, -5, 0])
    if k % 512:
        return np.exp2(np.random.permutation(np.resize(levels, k // 32))).repeat(32)
    a = np.empty((k // 512, 16))
    for p in range(k // 512):
        a[p, :8] = np.random.permutation(np.resize(levels, 8))
        for g in range(8):
            far = levels[np.abs(levels - a[p, g]) >= 10]
            a[p, g + 8] = far[np.random.randint(len(far))]
    return np.exp2(a.ravel()).repeat(32)


def f64(x):
    return np.asarray(x).astype(np.float64)


def striped(idx):
    return np.tile(idx.reshape(-1, 16).T, (8, 1)).astype(np.uint16)


def unstriped(offs):
    return offs[:16].T.reshape(-1).astype(np.int64)


def pack_weight(w):
    k, n = w.shape
    w = f64(np.asarray(w, np.float32).astype(ml_dtypes.bfloat16)).reshape(k // 32, 32, n)
    amax = np.abs(w).max(1)
    byte = np.clip(np.where(amax > 0, np.frexp(amax)[1] - 1 + 127 - 7, 1), 1, 254)
    scaled = (w * np.exp2(127.0 - byte)[:, None, :]).reshape(k, n).astype(np.float32)
    words = np.ascontiguousarray(scaled.reshape(k // 512, 128, 4, n).transpose(0, 1, 3, 2)).astype(ml_dtypes.float8_e4m3fn).view(np.uint8)
    return words, np.ascontiguousarray(byte.astype(np.uint8).reshape(k // 512, 16, n))


def unpack_weight(words, scales):
    g, p, n, _ = words.shape
    vals = np.ascontiguousarray(words).view(ml_dtypes.float8_e4m3fn).astype(np.float64) * np.repeat(np.exp2(scales.astype(np.float64) - 127.0), 8, axis=1)[..., None]
    return vals.transpose(0, 1, 3, 2).reshape(g * 512, n)


def planes(y):
    n, m = y.shape
    v = y.astype(np.float32).astype(ml_dtypes.bfloat16).astype(np.float64).reshape(n // 32, 32, m)
    top = np.abs(v).max(1)
    byte = np.clip(np.where(top > 0, np.frexp(top)[1] - 1 + 127 - 7, 1), 1, 254)
    codes = (v * np.exp2(127.0 - byte)[:, None, :]).reshape(n, m).astype(np.float32).astype(ml_dtypes.float8_e4m3fn).view(np.uint8)
    words = codes.reshape(n // 512, 128, 4, m).transpose(0, 1, 3, 2)
    return np.ascontiguousarray(words), np.ascontiguousarray(byte.astype(np.uint8).reshape(n // 512, 16, m))


def sigmoid(v):
    return 1.0 / (1.0 + np.exp(-np.maximum(v, -700.0)))


K, T, S, V, H, N, W = 512, 1024, 512, 256, 512, 512, 1024


def setup_inputs():
    n = np.random.standard_normal
    s = mx_kscale(K)[:, None]
    u = mx_kscale(H)
    near = np.random.permutation(S)
    far = np.random.permutation(S)
    packed_xT = pack_weight(n((K, T)) * s)
    packed_eT = pack_weight(n((K, W)) * s)
    packed_w2 = pack_weight(n((K, N)) / np.sqrt(K) / s)
    packed_w3 = pack_weight(n((H, N)) / np.sqrt(H) / u[:, None])
    return {
        "x_words": packed_xT[0],
        "x_scales": packed_xT[1],
        "e_words": packed_eT[0],
        "e_scales": packed_eT[1],
        "w1": (n((K, H)) / np.sqrt(K) / s * u).astype(np.float32),
        "w2_words": packed_w2[0],
        "w2_scales": packed_w2[1],
        "w3_words": packed_w3[0],
        "w3_scales": packed_w3[1],
        "offs": striped(np.random.permutation(T)[:S]),
        "pos1": striped(near[:V]),
        "pos2": striped(near[V:]),
        "attr": striped(np.random.permutation(W)[:S]),
        "edge1": striped(far[:V]),
        "edge2": striped(far[V:]),
    }


def reference(x_words, x_scales, e_words, e_scales, w1, w2_words, w2_scales, w3_words, w3_scales, offs, pos1, pos2, attr, edge1, edge2):
    e_attr = unpack_weight(e_words, e_scales)[:, unstriped(attr)]
    r = sigmoid(unpack_weight(w2_words, w2_scales).T @ e_attr)
    r0 = r[:, unstriped(edge1)]
    xq = unpack_weight(x_words, x_scales)[:, unstriped(offs)]
    h = mxq(f64(w1), 0, "e4m3").T @ xq
    r1 = r[:, unstriped(edge2)]
    z = r0 * h[:, unstriped(pos1)] + r1 * h[:, unstriped(pos2)]
    out_0 = unpack_weight(w3_words, w3_scales).T @ mxq(z, 0, "e4m3")
    return (out_0,) + planes(out_0)

@@ -1,0 +1,170 @@
+from contextlib import ExitStack
+
+import concourse.mybir as mybir
+
+K, T, S, V, H, N, W = 512, 1024, 512, 256, 512, 512, 1024
+FLOPS = 2 * K * H * S * 2 + 2 * H * N * V
+
+F32 = mybir.dt.float32
+BF16 = mybir.dt.bfloat16
+I32 = mybir.dt.int32
+U32 = mybir.dt.uint32
+U16 = mybir.dt.uint16
+U8 = mybir.dt.uint8
+FP8X4 = mybir.dt.float8_e4m3fn_x4
+ACT = mybir.ActivationFunctionType
+ALU = mybir.AluOpType
+
+P = 128
+PACK = 4
+PIECES = ((0, 128), (128, 128))
+
+
+def tile_picked_zcomp_sigmoid_po_kernel(tc, x_words, x_scales, e_words, e_scales, w1, w2_words, w2_scales, w3_words, w3_scales,
+        offs, pos1, pos2, attr, edge1, edge2, out_0, out_1, out_2):
+    nc = tc.nc
+    with ExitStack() as ctx:
+        sb = ctx.enter_context(tc.tile_pool(name="sb", bufs=1))
+        ps = ctx.enter_context(tc.psum_pool(name="ps", bufs=1))
+
+        def new(name, shape, dtype):
+            return sb.tile(shape, dtype, name=name, align_bytes=64)
+
+        def load_list(name, src):
+            t = new(name, list(src.shape), U16)
+            nc.sync.dma_start(t[:], src)
+            return t
+
+        def load_words(name, src):
+            t = new(name, [P, src.shape[2]], U32)
+            nc.sync.dma_start(t[:].bitcast(I32), src[0].rearrange("p n t -> p (n t)").bitcast(I32))
+            return t
+
+        def load_scales(name, src):
+            cols = src.shape[2]
+            t = new(name, [P, cols], U8)
+            rows = src[0].bitcast(I32)
+            for q in range(4):
+                nc.sync.dma_start(t[32 * q:32 * q + 32, :].bitcast(I32),
+                                  rows[4 * q:4 * q + 4, :].unsqueeze(0).broadcast_to([8, 4, cols // 4]))
+            return t
+
+        warm = new("warm", [P, 1], F32)
+        warm2 = new("warm2", [P, 1], F32)
+        nc.vector.memset(warm[:], 0.0)
+        nc.scalar.activation(warm2[:], warm[:], ACT.Sigmoid)
+
+        attr_t = load_list("attr_t", attr)
+        ew = load_words("ew", e_words)
+        es = load_scales("es", e_scales)
+        offs_t = load_list("offs_t", offs)
+        xw = load_words("xw", x_words)
+        w2w = load_words("w2w", w2_words)
+        w2s = load_scales("w2s", w2_scales)
+        w1raw = []
+        for u in range(2):
+            t = new("w1raw%d" % u, [P, PACK, H // 2], F32)
+            nc.sync.dma_start(t[:], w1.rearrange("(p j) c -> p j c", j=PACK)[:, :, u * (H // 2):(u + 1) * (H // 2)])
+            w1raw.append(t)
+        edge1_t = load_list("edge1_t", edge1)
+        xs = load_scales("xs", x_scales)
+        edges = [edge1_t, load_list("edge2_t", edge2)]
+        poss = [load_list("pos1_t", pos1), load_list("pos2_t", pos2)]
+        w3w = load_words("w3w", w3_words)
+        w3s = load_scales("w3s", w3_scales)
+
+        def deal(name, words, scales):
+            dw = new(name + "w", [P, 512], U32)
+            ds = new(name + "s", [P, 512], U8)
+            nc.vector.tensor_copy(dw[:].bitcast(I32).rearrange("p (t m) -> p m t", t=PACK),
+                                  words[:].bitcast(I32).rearrange("p (m t) -> p m t", t=PACK))
+            nc.vector.tensor_copy(ds[:].rearrange("p (t m) -> p m t", t=PACK),
+                                  scales[:].rearrange("p (m t) -> p m t", t=PACK))
+            return dw, ds
+
+        egw = new("egw", [P, S], U32)
+        egs = new("egs", [P, S], U8)
+        xgw = new("xgw", [P, S], U32)
+        xgs = new("xgs", [P, S], U8)
+        nc.vector.tensor_copy(egw[:], ew[:].indirect(attr_t[:]))
+        nc.vector.tensor_copy(egs[:], es[:].indirect(attr_t[:]))
+        nc.vector.tensor_copy(xgw[:], xw[:].indirect(offs_t[:]))
+        w2dw, w2ds = deal("w2d", w2w, w2s)
+        nc.vector.tensor_copy(xgs[:], xs[:].indirect(offs_t[:]))
+
+        r_t = []
+        for t in range(PACK):
+            bank = ps.tile([P, S], F32, name="rbank%d" % t, tag="r%d" % t)
+            cols = slice(t * P, (t + 1) * P)
+            nc.tensor.matmul_mx(out=bank[:], lhsT=w2dw[:, cols].bitcast(FP8X4), lhsT_scale=w2ds[:, cols],
+                                rhs=egw[:].bitcast(FP8X4), rhs_scale=egs[:], start=True, stop=True)
+            rt = new("r%d" % t, [P, S], F32)
+            nc.scalar.activation(rt[:], bank[:], ACT.Sigmoid)
+            r_t.append(rt)
+
+        w1b = new("w1b", [P, PACK, P, PACK], BF16)
+        for u in range(2):
+            nc.scalar.copy(w1b[:, :, u * 64:(u + 1) * 64, :].rearrange("p t m j -> p m j t"),
+                           w1raw[u][:].rearrange("p j (m t) -> p m j t", t=PACK))
+        w1w = new("w1w", [P, H], U32)
+        w1s = new("w1s", [P, H], U8)
+
+        rg = [new("rg%d" % d, [P, PACK, V], F32) for d in range(2)]
+        for t in range(PACK):
+            for d in range(2):
+                nc.vector.tensor_copy(rg[d][:, t, :], r_t[t][:].indirect(edges[d][:]))
+            if t == 1:
+                nc.vector.quantize_mx(out=w1w[:].bitcast(FP8X4), scales=w1s[:],
+                                      in_=w1b[:].rearrange("p t m j -> p (t m j)"))
+
+        h_t = []
+        for t in range(PACK):
+            bank = ps.tile([P, S], F32, name="hbank%d" % t, tag="h%d" % t)
+            cols = slice(t * P, (t + 1) * P)
+            nc.tensor.matmul_mx(out=bank[:], lhsT=w1w[:, cols].bitcast(FP8X4), lhsT_scale=w1s[:, cols],
+                                rhs=xgw[:].bitcast(FP8X4), rhs_scale=xgs[:], start=True, stop=True)
+            ht = new("h%d" % t, [P, S], F32)
+            nc.scalar.copy(ht[:], bank[:])
+            h_t.append(ht)
+
+        w3dw, w3ds = deal("w3d", w3w, w3s)
+
+        ys = new("ys", [P, V], U8)
+        out_rows = out_0.rearrange("(p t) v -> p t v", t=PACK)
+        out_words = out_1[0].rearrange("p n t -> p (n t)").bitcast(I32)
+        for a, (v0, n) in enumerate(PIECES):
+            last = a == len(PIECES) - 1
+            prod = [new("prod%d_%d" % (a, d), [P, PACK, n], F32) for d in range(2)]
+            for t in range(PACK):
+                for d in range(2):
+                    nc.vector.tensor_tensor(prod[d][:, t, :], h_t[t][:].indirect(poss[d][:, v0 // 16:(v0 + n) // 16]),
+                                            rg[d][:, t, v0:v0 + n], ALU.mult)
+            zb = new("zb%d" % a, [P, n, PACK], BF16)
+            nc.vector.tensor_tensor(zb[:].rearrange("p (c i) t -> p c t i", i=4),
+                                    prod[0][:].rearrange("p t (c i) -> p c t i", i=4),
+                                    prod[1][:].rearrange("p t (c i) -> p c t i", i=4), ALU.add)
+            zw = new("zw%d" % a, [P, n], U32)
+            zs = new("zs%d" % a, [P, n], U8)
+            nc.vector.quantize_mx(out=zw[:].bitcast(FP8X4), scales=zs[:], in_=zb[:].rearrange("p v t -> p (v t)"))
+            bank = ps.tile([P, PACK, n], F32, name="ybank%d" % a, tag="r%d" % a)
+            for t in range(PACK):
+                cols = slice(t * P, (t + 1) * P)
+                nc.tensor.matmul_mx(out=bank[:, t, :], lhsT=w3dw[:, cols].bitcast(FP8X4), lhsT_scale=w3ds[:, cols],
+                                    rhs=zw[:].bitcast(FP8X4), rhs_scale=zs[:], start=True, stop=True)
+            yb = new("yb%d" % a, [P, n, PACK], BF16)
+            y = new("y%d" % a, [P, PACK, n], F32)
+            if last:
+                nc.vector.tensor_copy(yb[:].rearrange("p (c i) t -> p c t i", i=4),
+                                      bank[:].rearrange("p t (c i) -> p c t i", i=4))
+                nc.scalar.copy(y[:], bank[:])
+            else:
+                nc.scalar.copy(y[:], bank[:])
+                nc.scalar.copy(yb[:].rearrange("p (c i) t -> p c t i", i=4),
+                               bank[:].rearrange("p t (c i) -> p c t i", i=4))
+            nc.sync.dma_start(out_rows[:, :, v0:v0 + n], y[:])
+            yw = new("yw%d" % a, [P, n], U32)
+            nc.vector.quantize_mx(out=yw[:].bitcast(FP8X4), scales=ys[:, v0:v0 + n], in_=yb[:].rearrange("p v t -> p (v t)"))
+            nc.sync.dma_start(out_words[:, v0:v0 + n], yw[:].bitcast(I32))
+        for r in range(4):
+            eng = nc.sync if r % 2 == 0 else nc.scalar
+            eng.dma_start(out_2[0].bitcast(I32)[r:16:4, :], ys[r:P:32, :].bitcast(I32))

@@ -17,7 +17,7 @@ ALU = mybir.AluOpType
 
 P = 128
 PACK = 4
-PIECES = ((0, 128), (128, 128))
+PIECES = ((0, (128, 64)), (192, (64,)))
 
 
 def tile_picked_zcomp_sigmoid_po_kernel(tc, x_words, x_scales, e_words, e_scales, w1, w2_words, w2_scales, w3_words, w3_scales,
@@ -27,8 +27,8 @@ def tile_picked_zcomp_sigmoid_po_kernel(tc, x_words, x_scales, e_words, e_scales
         sb = ctx.enter_context(tc.tile_pool(name="sb", bufs=1))
         ps = ctx.enter_context(tc.psum_pool(name="ps", bufs=1))
 
-        def new(name, shape, dtype):
-            return sb.tile(shape, dtype, name=name, align_bytes=64)
+        def new(name, shape, dtype, tag=None):
+            return sb.tile(shape, dtype, name=name, tag=tag or name, align_bytes=64)
 
         def load_list(name, src):
             t = new(name, list(src.shape), U16)
@@ -54,58 +54,64 @@ def tile_picked_zcomp_sigmoid_po_kernel(tc, x_words, x_scales, e_words, e_scales
         nc.vector.memset(warm[:], 0.0)
         nc.scalar.activation(warm2[:], warm[:], ACT.Sigmoid)
 
+        xs = new("xs", [P, T], U8)
+        w2s = new("w2s", [P, H], U8)
+        w3s = new("w3s", [P, N], U8)
+        for t in (w2s, xs, w3s):
+            nc.vector.memset(t[:].bitcast(I32), 0)
+
+        def load_scale_rows(t, src):
+            for r in range(4):
+                nc.sync.dma_start(t[r:P:32, :].bitcast(I32), src[0].bitcast(I32)[r:16:4, :])
+
         attr_t = load_list("attr_t", attr)
-        ew = load_words("ew", e_words)
         es = load_scales("es", e_scales)
-        offs_t = load_list("offs_t", offs)
-        xw = load_words("xw", x_words)
+        ew = load_words("ew", e_words)
         w2w = load_words("w2w", w2_words)
-        w2s = load_scales("w2s", w2_scales)
-        w1raw = []
-        for u in range(2):
-            t = new("w1raw%d" % u, [P, PACK, H // 2], F32)
-            nc.sync.dma_start(t[:], w1.rearrange("(p j) c -> p j c", j=PACK)[:, :, u * (H // 2):(u + 1) * (H // 2)])
-            w1raw.append(t)
-        edge1_t = load_list("edge1_t", edge1)
-        xs = load_scales("xs", x_scales)
-        edges = [edge1_t, load_list("edge2_t", edge2)]
+        offs_t = load_list("offs_t", offs)
+        load_scale_rows(w2s, w2_scales)
+        xw = load_words("xw", x_words)
+        w1raw = new("w1raw", [P, PACK, H], F32)
+        nc.sync.dma_start(w1raw[:], w1.rearrange("(p j) c -> p j c", j=PACK))
+        edges = [load_list("edge1_t", edge1), load_list("edge2_t", edge2)]
+        load_scale_rows(xs, x_scales)
+        load_scale_rows(w3s, w3_scales)
         poss = [load_list("pos1_t", pos1), load_list("pos2_t", pos2)]
         w3w = load_words("w3w", w3_words)
-        w3s = load_scales("w3s", w3_scales)
 
-        def deal(name, words, scales):
-            dw = new(name + "w", [P, 512], U32)
-            ds = new(name + "s", [P, 512], U8)
-            nc.vector.tensor_copy(dw[:].bitcast(I32).rearrange("p (t m) -> p m t", t=PACK),
-                                  words[:].bitcast(I32).rearrange("p (m t) -> p m t", t=PACK))
-            nc.vector.tensor_copy(ds[:].rearrange("p (t m) -> p m t", t=PACK),
-                                  scales[:].rearrange("p (m t) -> p m t", t=PACK))
-            return dw, ds
+        def deal(name, src, dtype, tag=None):
+            dst = new(name, [P, 512], dtype, tag)
+            a, b = (dst[:], src[:]) if dtype == U8 else (dst[:].bitcast(I32), src[:].bitcast(I32))
+            nc.vector.tensor_copy(a.rearrange("p (t m) -> p m t", t=PACK), b.rearrange("p (m t) -> p m t", t=PACK))
+            return dst
 
         egw = new("egw", [P, S], U32)
         egs = new("egs", [P, S], U8)
         xgw = new("xgw", [P, S], U32)
-        xgs = new("xgs", [P, S], U8)
-        nc.vector.tensor_copy(egw[:], ew[:].indirect(attr_t[:]))
         nc.vector.tensor_copy(egs[:], es[:].indirect(attr_t[:]))
+        nc.vector.tensor_copy(egw[:], ew[:].indirect(attr_t[:]))
+        w2dw = deal("w2dw", w2w, U32)
+        w2ds = deal("w2ds", w2s, U8)
         nc.vector.tensor_copy(xgw[:], xw[:].indirect(offs_t[:]))
-        w2dw, w2ds = deal("w2d", w2w, w2s)
-        nc.vector.tensor_copy(xgs[:], xs[:].indirect(offs_t[:]))
 
-        r_t = []
+        rbanks = []
         for t in range(PACK):
             bank = ps.tile([P, S], F32, name="rbank%d" % t, tag="r%d" % t)
             cols = slice(t * P, (t + 1) * P)
             nc.tensor.matmul_mx(out=bank[:], lhsT=w2dw[:, cols].bitcast(FP8X4), lhsT_scale=w2ds[:, cols],
                                 rhs=egw[:].bitcast(FP8X4), rhs_scale=egs[:], start=True, stop=True)
-            rt = new("r%d" % t, [P, S], F32)
-            nc.scalar.activation(rt[:], bank[:], ACT.Sigmoid)
-            r_t.append(rt)
+            rbanks.append(bank)
 
-        w1b = new("w1b", [P, PACK, P, PACK], BF16)
-        for u in range(2):
-            nc.scalar.copy(w1b[:, :, u * 64:(u + 1) * 64, :].rearrange("p t m j -> p m j t"),
-                           w1raw[u][:].rearrange("p j (m t) -> p m j t", t=PACK))
+        w1b = new("w1b", [P, PACK, P, PACK], BF16, "w2dw")
+        r_t = []
+        for t in range(PACK):
+            rt = new("r%d" % t, [P, S], F32)
+            nc.scalar.activation(rt[:], rbanks[t][:], ACT.Sigmoid)
+            r_t.append(rt)
+            if t in (1, 2):
+                u = t - 1
+                nc.scalar.copy(w1b[:, :, u * 64:(u + 1) * 64, :].rearrange("p t m j -> p m j t"),
+                               w1raw[:, :, u * 256:(u + 1) * 256].rearrange("p j (m t) -> p m j t", t=PACK))
         w1w = new("w1w", [P, H], U32)
         w1s = new("w1s", [P, H], U8)
 
@@ -114,6 +120,9 @@ def tile_picked_zcomp_sigmoid_po_kernel(tc, x_words, x_scales, e_words, e_scales
             for d in range(2):
                 nc.vector.tensor_copy(rg[d][:, t, :], r_t[t][:].indirect(edges[d][:]))
             if t == 1:
+                xgs = new("xgs", [P, S], U8, "r1")
+                nc.vector.tensor_copy(xgs[:], xs[:].indirect(offs_t[:]))
+            if t == 2:
                 nc.vector.quantize_mx(out=w1w[:].bitcast(FP8X4), scales=w1s[:],
                                       in_=w1b[:].rearrange("p t m j -> p (t m j)"))
 
@@ -127,13 +136,16 @@ def tile_picked_zcomp_sigmoid_po_kernel(tc, x_words, x_scales, e_words, e_scales
             nc.scalar.copy(ht[:], bank[:])
             h_t.append(ht)
 
-        w3dw, w3ds = deal("w3d", w3w, w3s)
+        w3dw = deal("w3dw", w3w, U32, "r3")
+        w3ds = deal("w3ds", w3s, U8, "r2")
 
         ys = new("ys", [P, V], U8)
+        yw = new("yw", [P, V], U32)
         out_rows = out_0.rearrange("(p t) v -> p t v", t=PACK)
         out_words = out_1[0].rearrange("p n t -> p (n t)").bitcast(I32)
-        for a, (v0, n) in enumerate(PIECES):
+        for a, (v0, widths) in enumerate(PIECES):
             last = a == len(PIECES) - 1
+            n = sum(widths)
             prod = [new("prod%d_%d" % (a, d), [P, PACK, n], F32) for d in range(2)]
             for t in range(PACK):
                 for d in range(2):
@@ -143,28 +155,32 @@ def tile_picked_zcomp_sigmoid_po_kernel(tc, x_words, x_scales, e_words, e_scales
             nc.vector.tensor_tensor(zb[:].rearrange("p (c i) t -> p c t i", i=4),
                                     prod[0][:].rearrange("p t (c i) -> p c t i", i=4),
                                     prod[1][:].rearrange("p t (c i) -> p c t i", i=4), ALU.add)
-            zw = new("zw%d" % a, [P, n], U32)
-            zs = new("zs%d" % a, [P, n], U8)
-            nc.vector.quantize_mx(out=zw[:].bitcast(FP8X4), scales=zs[:], in_=zb[:].rearrange("p v t -> p (v t)"))
-            bank = ps.tile([P, PACK, n], F32, name="ybank%d" % a, tag="r%d" % a)
-            for t in range(PACK):
-                cols = slice(t * P, (t + 1) * P)
-                nc.tensor.matmul_mx(out=bank[:, t, :], lhsT=w3dw[:, cols].bitcast(FP8X4), lhsT_scale=w3ds[:, cols],
-                                    rhs=zw[:].bitcast(FP8X4), rhs_scale=zs[:], start=True, stop=True)
-            yb = new("yb%d" % a, [P, n, PACK], BF16)
-            y = new("y%d" % a, [P, PACK, n], F32)
-            if last:
-                nc.vector.tensor_copy(yb[:].rearrange("p (c i) t -> p c t i", i=4),
-                                      bank[:].rearrange("p t (c i) -> p c t i", i=4))
-                nc.scalar.copy(y[:], bank[:])
-            else:
-                nc.scalar.copy(y[:], bank[:])
-                nc.scalar.copy(yb[:].rearrange("p (c i) t -> p c t i", i=4),
-                               bank[:].rearrange("p t (c i) -> p c t i", i=4))
-            nc.sync.dma_start(out_rows[:, :, v0:v0 + n], y[:])
-            yw = new("yw%d" % a, [P, n], U32)
-            nc.vector.quantize_mx(out=yw[:].bitcast(FP8X4), scales=ys[:, v0:v0 + n], in_=yb[:].rearrange("p v t -> p (v t)"))
-            nc.sync.dma_start(out_words[:, v0:v0 + n], yw[:].bitcast(I32))
+            c0 = 0
+            for m in widths:
+                b = v0 + c0
+                zw = new("zw%d" % b, [P, m], U32)
+                zs = new("zs%d" % b, [P, m], U8)
+                nc.vector.quantize_mx(out=zw[:].bitcast(FP8X4), scales=zs[:],
+                                      in_=zb[:, c0:c0 + m, :].rearrange("p v t -> p (v t)"))
+                bank = ps.tile([P, PACK, m], F32, name="ybank%d" % b, tag="r%d" % (b // 64 % 4))
+                for t in range(PACK):
+                    cols = slice(t * P, (t + 1) * P)
+                    nc.tensor.matmul_mx(out=bank[:, t, :], lhsT=w3dw[:, cols].bitcast(FP8X4), lhsT_scale=w3ds[:, cols],
+                                        rhs=zw[:].bitcast(FP8X4), rhs_scale=zs[:], start=True, stop=True)
+                yb = new("yb%d" % b, [P, m, PACK], BF16)
+                y = new("y%d" % b, [P, PACK, m], F32)
+                if last:
+                    nc.vector.tensor_copy(yb[:].rearrange("p (c i) t -> p c t i", i=4),
+                                          bank[:].rearrange("p t (c i) -> p c t i", i=4))
+                    nc.scalar.copy(y[:], bank[:])
+                else:
+                    nc.scalar.copy(yb[:].rearrange("p (c i) t -> p c t i", i=4),
+                                   bank[:].rearrange("p t (c i) -> p c t i", i=4))
+                    nc.scalar.copy(y[:], bank[:])
+                (nc.scalar if last else nc.sync).dma_start(out_rows[:, :, b:b + m], y[:])
+                nc.vector.quantize_mx(out=yw[:, b:b + m].bitcast(FP8X4), scales=ys[:, b:b + m], in_=yb[:].rearrange("p v t -> p (v t)"))
+                c0 = c0 + m
+            nc.sync.dma_start(out_words[:, v0:v0 + n], yw[:, v0:v0 + n].bitcast(I32))
         for r in range(4):
-            eng = nc.sync if r % 2 == 0 else nc.scalar
+            eng = nc.sync if r < 3 else nc.scalar
             eng.dma_start(out_2[0].bitcast(I32)[r:16:4, :], ys[r:P:32, :].bitcast(I32))

@@ -71,10 +71,10 @@ def tile_picked_zcomp_sigmoid_po_kernel(tc, x_words, x_scales, e_words, e_scales
         offs_t = load_list("offs_t", offs)
         load_scale_rows(w2s, w2_scales)
         xw = load_words("xw", x_words)
+        load_scale_rows(xs, x_scales)
+        edges = [load_list("edge1_t", edge1), load_list("edge2_t", edge2)]
         w1raw = new("w1raw", [P, PACK, H], F32)
         nc.sync.dma_start(w1raw[:], w1.rearrange("(p j) c -> p j c", j=PACK))
-        edges = [load_list("edge1_t", edge1), load_list("edge2_t", edge2)]
-        load_scale_rows(xs, x_scales)
         load_scale_rows(w3s, w3_scales)
         poss = [load_list("pos1_t", pos1), load_list("pos2_t", pos2)]
         w3w = load_words("w3w", w3_words)
@@ -93,6 +93,8 @@ def tile_picked_zcomp_sigmoid_po_kernel(tc, x_words, x_scales, e_words, e_scales
         w2dw = deal("w2dw", w2w, U32)
         w2ds = deal("w2ds", w2s, U8)
         nc.vector.tensor_copy(xgw[:], xw[:].indirect(offs_t[:]))
+        xgs = new("xgs", [P, S], U8)
+        nc.vector.tensor_copy(xgs[:], xs[:].indirect(offs_t[:]))
 
         rbanks = []
         for t in range(PACK):
@@ -108,20 +110,18 @@ def tile_picked_zcomp_sigmoid_po_kernel(tc, x_words, x_scales, e_words, e_scales
             rt = new("r%d" % t, [P, S], F32)
             nc.scalar.activation(rt[:], rbanks[t][:], ACT.Sigmoid)
             r_t.append(rt)
-            if t in (1, 2):
-                u = t - 1
-                nc.scalar.copy(w1b[:, :, u * 64:(u + 1) * 64, :].rearrange("p t m j -> p m j t"),
-                               w1raw[:, :, u * 256:(u + 1) * 256].rearrange("p j (m t) -> p m j t", t=PACK))
+            if t == 3:
+                for u in range(2):
+                    nc.scalar.copy(w1b[:, 2 * u:2 * u + 2, :, :].rearrange("p t m j -> p m j t"),
+                                   w1raw[:].rearrange("p j (m t) -> p m j t", t=PACK)[:, :, :, 2 * u:2 * u + 2])
         w1w = new("w1w", [P, H], U32)
         w1s = new("w1s", [P, H], U8)
 
-        rg = [new("rg%d" % d, [P, PACK, V], F32) for d in range(2)]
+        rg = []
         for t in range(PACK):
+            rg.append(new("rg%d" % t, [P, 2, V], F32, "w1raw" if t == 3 else None))
             for d in range(2):
-                nc.vector.tensor_copy(rg[d][:, t, :], r_t[t][:].indirect(edges[d][:]))
-            if t == 1:
-                xgs = new("xgs", [P, S], U8, "r1")
-                nc.vector.tensor_copy(xgs[:], xs[:].indirect(offs_t[:]))
+                nc.vector.tensor_copy(rg[t][:, d, :], r_t[t][:].indirect(edges[d][:]))
             if t == 2:
                 nc.vector.quantize_mx(out=w1w[:].bitcast(FP8X4), scales=w1s[:],
                                       in_=w1b[:].rearrange("p t m j -> p (t m j)"))
@@ -146,15 +146,15 @@ def tile_picked_zcomp_sigmoid_po_kernel(tc, x_words, x_scales, e_words, e_scales
         for a, (v0, widths) in enumerate(PIECES):
             last = a == len(PIECES) - 1
             n = sum(widths)
-            prod = [new("prod%d_%d" % (a, d), [P, PACK, n], F32) for d in range(2)]
+            prod = [new("prod%d_%d" % (a, d), [P, PACK, n], F32, "prod%d" % d) for d in range(2)]
             for t in range(PACK):
                 for d in range(2):
                     nc.vector.tensor_tensor(prod[d][:, t, :], h_t[t][:].indirect(poss[d][:, v0 // 16:(v0 + n) // 16]),
-                                            rg[d][:, t, v0:v0 + n], ALU.mult)
+                                            rg[t][:, d, v0:v0 + n], ALU.mult)
             zb = new("zb%d" % a, [P, n, PACK], BF16)
-            nc.vector.tensor_tensor(zb[:].rearrange("p (c i) t -> p c t i", i=4),
-                                    prod[0][:].rearrange("p t (c i) -> p c t i", i=4),
-                                    prod[1][:].rearrange("p t (c i) -> p c t i", i=4), ALU.add)
+            nc.vector.tensor_tensor(zb[:].rearrange("p (c i) t -> p c t i", i=2),
+                                    prod[0][:].rearrange("p t (c i) -> p c t i", i=2),
+                                    prod[1][:].rearrange("p t (c i) -> p c t i", i=2), ALU.add)
             c0 = 0
             for m in widths:
                 b = v0 + c0
@@ -162,25 +162,30 @@ def tile_picked_zcomp_sigmoid_po_kernel(tc, x_words, x_scales, e_words, e_scales
                 zs = new("zs%d" % b, [P, m], U8)
                 nc.vector.quantize_mx(out=zw[:].bitcast(FP8X4), scales=zs[:],
                                       in_=zb[:, c0:c0 + m, :].rearrange("p v t -> p (v t)"))
-                bank = ps.tile([P, PACK, m], F32, name="ybank%d" % b, tag="r%d" % (b // 64 % 4))
-                for t in range(PACK):
-                    cols = slice(t * P, (t + 1) * P)
-                    nc.tensor.matmul_mx(out=bank[:, t, :], lhsT=w3dw[:, cols].bitcast(FP8X4), lhsT_scale=w3ds[:, cols],
-                                        rhs=zw[:].bitcast(FP8X4), rhs_scale=zs[:], start=True, stop=True)
                 yb = new("yb%d" % b, [P, m, PACK], BF16)
                 y = new("y%d" % b, [P, PACK, m], F32)
+                nb = 2 if last else 1
+                per = PACK // nb
+                banks = [ps.tile([P, per, m], F32, name="ybank%d_%d" % (b, k), tag="r%d" % ((b // 64 - k * 2) % 4)) for k in range(nb)]
+                for t in range(PACK):
+                    cols = slice(t * P, (t + 1) * P)
+                    nc.tensor.matmul_mx(out=banks[t // per][:, t % per, :], lhsT=w3dw[:, cols].bitcast(FP8X4), lhsT_scale=w3ds[:, cols],
+                                        rhs=zw[:].bitcast(FP8X4), rhs_scale=zs[:], start=True, stop=True)
                 if last:
-                    nc.vector.tensor_copy(yb[:].rearrange("p (c i) t -> p c t i", i=4),
-                                          bank[:].rearrange("p t (c i) -> p c t i", i=4))
-                    nc.scalar.copy(y[:], bank[:])
+                    for k in range(nb):
+                        rows = slice(k * per, (k + 1) * per)
+                        nc.vector.tensor_copy(yb[:, :, rows].rearrange("p (c i) t -> p c t i", i=2),
+                                              banks[k][:].rearrange("p t (c i) -> p c t i", i=2))
+                        nc.scalar.copy(y[:, rows, :], banks[k][:])
+                        (nc.scalar if k else nc.sync).dma_start(out_rows[:, rows, b:b + m], y[:, rows, :])
                 else:
-                    nc.scalar.copy(yb[:].rearrange("p (c i) t -> p c t i", i=4),
-                                   bank[:].rearrange("p t (c i) -> p c t i", i=4))
-                    nc.scalar.copy(y[:], bank[:])
-                (nc.scalar if last else nc.sync).dma_start(out_rows[:, :, b:b + m], y[:])
+                    nc.scalar.copy(yb[:].rearrange("p (c i) t -> p c t i", i=2),
+                                   banks[0][:].rearrange("p t (c i) -> p c t i", i=2))
+                    nc.scalar.copy(y[:], banks[0][:])
+                    nc.sync.dma_start(out_rows[:, :, b:b + m], y[:])
                 nc.vector.quantize_mx(out=yw[:, b:b + m].bitcast(FP8X4), scales=ys[:, b:b + m], in_=yb[:].rearrange("p v t -> p (v t)"))
                 c0 = c0 + m
-            nc.sync.dma_start(out_words[:, v0:v0 + n], yw[:, v0:v0 + n].bitcast(I32))
+        nc.sync.dma_start(out_words, yw[:].bitcast(I32))
         for r in range(4):
-            eng = nc.sync if r < 3 else nc.scalar
+            eng = nc.sync if r < 2 else nc.scalar
             eng.dma_start(out_2[0].bitcast(I32)[r:16:4, :], ys[r:P:32, :].bitcast(I32))

@@ -17,7 +17,7 @@ ALU = mybir.AluOpType
 
 P = 128
 PACK = 4
-PIECES = ((0, (128, 64)), (192, (64,)))
+HALF = V // 2
 
 
 def tile_picked_zcomp_sigmoid_po_kernel(tc, x_words, x_scales, e_words, e_scales, w1, w2_words, w2_scales, w3_words, w3_scales,
@@ -64,127 +64,148 @@ def tile_picked_zcomp_sigmoid_po_kernel(tc, x_words, x_scales, e_words, e_scales
             for r in range(4):
                 nc.sync.dma_start(t[r:P:32, :].bitcast(I32), src[0].bitcast(I32)[r:16:4, :])
 
+        w1rows = w1.rearrange("(p j) c -> p j c", j=PACK)
+
+        def load_w1(u):
+            t = new("w1raw%d" % u, [P, PACK, H // 2], F32)
+            nc.sync.dma_start(t[:], w1rows[:, :, u * (H // 2):(u + 1) * (H // 2)])
+            return t
+
         attr_t = load_list("attr_t", attr)
         es = load_scales("es", e_scales)
         ew = load_words("ew", e_words)
         w2w = load_words("w2w", w2_words)
-        offs_t = load_list("offs_t", offs)
         load_scale_rows(w2s, w2_scales)
+        w1raw = [load_w1(0)]
+        offs_t = load_list("offs_t", offs)
         xw = load_words("xw", x_words)
-        load_scale_rows(xs, x_scales)
         edges = [load_list("edge1_t", edge1), load_list("edge2_t", edge2)]
-        w1raw = new("w1raw", [P, PACK, H], F32)
-        nc.sync.dma_start(w1raw[:], w1.rearrange("(p j) c -> p j c", j=PACK))
-        load_scale_rows(w3s, w3_scales)
+        load_scale_rows(xs, x_scales)
+        w1raw.append(load_w1(1))
         poss = [load_list("pos1_t", pos1), load_list("pos2_t", pos2)]
         w3w = load_words("w3w", w3_words)
+        load_scale_rows(w3s, w3_scales)
 
-        def deal(name, src, dtype, tag=None):
-            dst = new(name, [P, 512], dtype, tag)
-            a, b = (dst[:], src[:]) if dtype == U8 else (dst[:].bitcast(I32), src[:].bitcast(I32))
-            nc.vector.tensor_copy(a.rearrange("p (t m) -> p m t", t=PACK), b.rearrange("p (m t) -> p m t", t=PACK))
+        def deal(name, src, dtype):
+            dst = new(name, [P, 512], dtype)
+            nc.gpsimd.tensor_copy(dst[:].rearrange("p (t c i) -> p c t i", t=PACK, i=4),
+                                  src[:].rearrange("p (c i t) -> p c t i", t=PACK, i=4))
             return dst
 
         egw = new("egw", [P, S], U32)
         egs = new("egs", [P, S], U8)
         xgw = new("xgw", [P, S], U32)
+        xgs = new("xgs", [P, S], U8)
         nc.vector.tensor_copy(egs[:], es[:].indirect(attr_t[:]))
         nc.vector.tensor_copy(egw[:], ew[:].indirect(attr_t[:]))
         w2dw = deal("w2dw", w2w, U32)
         w2ds = deal("w2ds", w2s, U8)
-        nc.vector.tensor_copy(xgw[:], xw[:].indirect(offs_t[:]))
-        xgs = new("xgs", [P, S], U8)
-        nc.vector.tensor_copy(xgs[:], xs[:].indirect(offs_t[:]))
+        w3dw = deal("w3dw", w3w, U32)
+        w3ds = deal("w3ds", w3s, U8)
 
-        rbanks = []
+        w1b = new("w1b", [P, PACK, P, PACK], BF16)
+
+        def round_w1(u):
+            nc.vector.tensor_copy(w1b[:, :, u * 64:(u + 1) * 64, :].rearrange("p t m j -> p m j t"),
+                                  w1raw[u][:].rearrange("p j (m t) -> p m j t", t=PACK))
+
+        round_w1(0)
+        nc.vector.tensor_copy(xgw[:], xw[:].indirect(offs_t[:]))
+        nc.vector.tensor_copy(xgs[:], xs[:].indirect(offs_t[:]))
+        round_w1(1)
+
+        r_t = []
+        rg = {}
+
+        def edge_gathers(t, tag=None):
+            rg[t] = new("rg%d" % t, [P, 2, V], F32, tag)
+            for d in range(2):
+                nc.scalar.activation(rg[t][:, d, :], r_t[t][:].indirect(edges[d][:]), ACT.Sigmoid)
+
         for t in range(PACK):
             bank = ps.tile([P, S], F32, name="rbank%d" % t, tag="r%d" % t)
             cols = slice(t * P, (t + 1) * P)
             nc.tensor.matmul_mx(out=bank[:], lhsT=w2dw[:, cols].bitcast(FP8X4), lhsT_scale=w2ds[:, cols],
                                 rhs=egw[:].bitcast(FP8X4), rhs_scale=egs[:], start=True, stop=True)
-            rbanks.append(bank)
-
-        w1b = new("w1b", [P, PACK, P, PACK], BF16, "w2dw")
-        r_t = []
-        for t in range(PACK):
             rt = new("r%d" % t, [P, S], F32)
-            nc.scalar.activation(rt[:], rbanks[t][:], ACT.Sigmoid)
+            nc.scalar.copy(rt[:], bank[:])
             r_t.append(rt)
-            if t == 3:
-                for u in range(2):
-                    nc.scalar.copy(w1b[:, 2 * u:2 * u + 2, :, :].rearrange("p t m j -> p m j t"),
-                                   w1raw[:].rearrange("p j (m t) -> p m j t", t=PACK)[:, :, :, 2 * u:2 * u + 2])
-        w1w = new("w1w", [P, H], U32)
-        w1s = new("w1s", [P, H], U8)
+            if t < 2:
+                edge_gathers(t)
 
-        rg = []
-        for t in range(PACK):
-            rg.append(new("rg%d" % t, [P, 2, V], F32, "w1raw" if t == 3 else None))
+        hbanks = []
+        for u in range(2):
+            w1w = new("w1w%d" % u, [P, 2 * P], U32)
+            w1s = new("w1s%d" % u, [P, 2 * P], U8)
+            nc.vector.quantize_mx(out=w1w[:].bitcast(FP8X4), scales=w1s[:],
+                                  in_=w1b[:, 2 * u:2 * u + 2, :, :].rearrange("p t m j -> p (t m j)"))
+            for i in range(2):
+                t = 2 * u + i
+                bank = ps.tile([P, S], F32, name="hbank%d" % t, tag="h%d" % t)
+                cols = slice(i * P, (i + 1) * P)
+                nc.tensor.matmul_mx(out=bank[:], lhsT=w1w[:, cols].bitcast(FP8X4), lhsT_scale=w1s[:, cols],
+                                    rhs=xgw[:].bitcast(FP8X4), rhs_scale=xgs[:], start=True, stop=True)
+                hbanks.append(bank)
+
+        h_t = [new("h%d" % t, [P, S], F32) for t in range(PACK)]
+        nc.vector.tensor_copy(h_t[0][:], hbanks[0][:])
+        nc.scalar.copy(h_t[1][:], hbanks[1][:])
+        edge_gathers(2, "w1w0")
+        nc.scalar.copy(h_t[2][:], hbanks[2][:])
+        edge_gathers(3, "w1w1")
+        nc.scalar.copy(h_t[3][:], hbanks[3][:])
+
+        prod = [new("prod%d" % d, [P, PACK, V], F32) for d in range(2)]
+
+        def node_gathers(t, v0, n):
             for d in range(2):
-                nc.vector.tensor_copy(rg[t][:, d, :], r_t[t][:].indirect(edges[d][:]))
-            if t == 2:
-                nc.vector.quantize_mx(out=w1w[:].bitcast(FP8X4), scales=w1s[:],
-                                      in_=w1b[:].rearrange("p t m j -> p (t m j)"))
+                nc.vector.tensor_tensor(prod[d][:, t, v0:v0 + n], h_t[t][:].indirect(poss[d][:, v0 // 16:(v0 + n) // 16]),
+                                        rg[t][:, d, v0:v0 + n], ALU.mult)
 
-        h_t = []
-        for t in range(PACK):
-            bank = ps.tile([P, S], F32, name="hbank%d" % t, tag="h%d" % t)
-            cols = slice(t * P, (t + 1) * P)
-            nc.tensor.matmul_mx(out=bank[:], lhsT=w1w[:, cols].bitcast(FP8X4), lhsT_scale=w1s[:, cols],
-                                rhs=xgw[:].bitcast(FP8X4), rhs_scale=xgs[:], start=True, stop=True)
-            ht = new("h%d" % t, [P, S], F32)
-            nc.scalar.copy(ht[:], bank[:])
-            h_t.append(ht)
-
-        w3dw = deal("w3dw", w3w, U32, "r3")
-        w3ds = deal("w3ds", w3s, U8, "r2")
+        for t in range(PACK - 1):
+            node_gathers(t, 0, V)
 
         ys = new("ys", [P, V], U8)
         yw = new("yw", [P, V], U32)
         out_rows = out_0.rearrange("(p t) v -> p t v", t=PACK)
         out_words = out_1[0].rearrange("p n t -> p (n t)").bitcast(I32)
-        for a, (v0, widths) in enumerate(PIECES):
-            last = a == len(PIECES) - 1
-            n = sum(widths)
-            prod = [new("prod%d_%d" % (a, d), [P, PACK, n], F32, "prod%d" % d) for d in range(2)]
-            for t in range(PACK):
-                for d in range(2):
-                    nc.vector.tensor_tensor(prod[d][:, t, :], h_t[t][:].indirect(poss[d][:, v0 // 16:(v0 + n) // 16]),
-                                            rg[t][:, d, v0:v0 + n], ALU.mult)
-            zb = new("zb%d" % a, [P, n, PACK], BF16)
+        zq = []
+        for a in range(2):
+            v0 = a * HALF
+            node_gathers(PACK - 1, v0, HALF)
+            zb = new("zb%d" % a, [P, HALF, PACK], BF16)
             nc.vector.tensor_tensor(zb[:].rearrange("p (c i) t -> p c t i", i=2),
-                                    prod[0][:].rearrange("p t (c i) -> p c t i", i=2),
-                                    prod[1][:].rearrange("p t (c i) -> p c t i", i=2), ALU.add)
-            c0 = 0
-            for m in widths:
-                b = v0 + c0
-                zw = new("zw%d" % b, [P, m], U32)
-                zs = new("zs%d" % b, [P, m], U8)
-                nc.vector.quantize_mx(out=zw[:].bitcast(FP8X4), scales=zs[:],
-                                      in_=zb[:, c0:c0 + m, :].rearrange("p v t -> p (v t)"))
-                yb = new("yb%d" % b, [P, m, PACK], BF16)
-                y = new("y%d" % b, [P, PACK, m], F32)
-                nb = 2 if last else 1
-                per = PACK // nb
-                banks = [ps.tile([P, per, m], F32, name="ybank%d_%d" % (b, k), tag="r%d" % ((b // 64 - k * 2) % 4)) for k in range(nb)]
-                for t in range(PACK):
-                    cols = slice(t * P, (t + 1) * P)
-                    nc.tensor.matmul_mx(out=banks[t // per][:, t % per, :], lhsT=w3dw[:, cols].bitcast(FP8X4), lhsT_scale=w3ds[:, cols],
-                                        rhs=zw[:].bitcast(FP8X4), rhs_scale=zs[:], start=True, stop=True)
-                if last:
-                    for k in range(nb):
-                        rows = slice(k * per, (k + 1) * per)
-                        nc.vector.tensor_copy(yb[:, :, rows].rearrange("p (c i) t -> p c t i", i=2),
-                                              banks[k][:].rearrange("p t (c i) -> p c t i", i=2))
-                        nc.scalar.copy(y[:, rows, :], banks[k][:])
-                        (nc.scalar if k else nc.sync).dma_start(out_rows[:, rows, b:b + m], y[:, rows, :])
-                else:
-                    nc.scalar.copy(yb[:].rearrange("p (c i) t -> p c t i", i=2),
-                                   banks[0][:].rearrange("p t (c i) -> p c t i", i=2))
-                    nc.scalar.copy(y[:], banks[0][:])
-                    nc.sync.dma_start(out_rows[:, :, b:b + m], y[:])
-                nc.vector.quantize_mx(out=yw[:, b:b + m].bitcast(FP8X4), scales=ys[:, b:b + m], in_=yb[:].rearrange("p v t -> p (v t)"))
-                c0 = c0 + m
+                                    prod[0][:, :, v0:v0 + HALF].rearrange("p t (c i) -> p c t i", i=2),
+                                    prod[1][:, :, v0:v0 + HALF].rearrange("p t (c i) -> p c t i", i=2), ALU.add)
+            zw = new("zw%d" % a, [P, HALF], U32)
+            zs = new("zs%d" % a, [P, HALF], U8)
+            nc.vector.quantize_mx(out=zw[:].bitcast(FP8X4), scales=zs[:], in_=zb[:].rearrange("p v t -> p (v t)"))
+            zq.append((zw, zs))
+        for a in range(2):
+            v0 = a * HALF
+            zw, zs = zq[a]
+            yb = new("yb%d" % a, [P, HALF, PACK], BF16)
+            y = new("y%d" % a, [P, PACK, HALF], F32)
+            nb = 1 + a
+            per = PACK // nb
+            banks = [ps.tile([P, per, HALF], F32, name="ybank%d_%d" % (a, k), tag="r%d" % (a + k)) for k in range(nb)]
+            for t in range(PACK):
+                cols = slice(t * P, (t + 1) * P)
+                nc.tensor.matmul_mx(out=banks[t // per][:, t % per, :], lhsT=w3dw[:, cols].bitcast(FP8X4), lhsT_scale=w3ds[:, cols],
+                                    rhs=zw[:].bitcast(FP8X4), rhs_scale=zs[:], start=True, stop=True)
+            if a == 0:
+                nc.scalar.copy(yb[:].rearrange("p (c i) t -> p c t i", i=2),
+                               banks[0][:].rearrange("p t (c i) -> p c t i", i=2))
+                nc.scalar.copy(y[:], banks[0][:])
+                nc.sync.dma_start(out_rows[:, :, v0:v0 + HALF], y[:])
+            else:
+                for k in range(nb):
+                    rows = slice(k * per, (k + 1) * per)
+                    nc.vector.tensor_copy(yb[:, :, rows].rearrange("p (c i) t -> p c t i", i=2),
+                                          banks[k][:].rearrange("p t (c i) -> p c t i", i=2))
+                    nc.scalar.copy(y[:, rows, :], banks[k][:])
+                    (nc.scalar if k else nc.sync).dma_start(out_rows[:, rows, v0:v0 + HALF], y[:, rows, :])
+            nc.vector.quantize_mx(out=yw[:, v0:v0 + HALF].bitcast(FP8X4), scales=ys[:, v0:v0 + HALF], in_=yb[:].rearrange("p v t -> p (v t)"))
         nc.sync.dma_start(out_words, yw[:].bitcast(I32))
         for r in range(4):
             eng = nc.sync if r < 2 else nc.scalar

@@ -57,12 +57,13 @@ def tile_picked_zcomp_sigmoid_po_kernel(tc, x_words, x_scales, e_words, e_scales
         xs = new("xs", [P, T], U8)
         w2s = new("w2s", [P, H], U8)
         w3s = new("w3s", [P, N], U8)
-        for t in (w2s, xs, w3s):
+        nc.gpsimd.memset(xs[:].bitcast(I32), 0)
+        for t in (w2s, w3s):
             nc.vector.memset(t[:].bitcast(I32), 0)
 
-        def load_scale_rows(t, src):
+        def load_scale_rows(t, src, eng=nc.sync):
             for r in range(4):
-                nc.sync.dma_start(t[r:P:32, :].bitcast(I32), src[0].bitcast(I32)[r:16:4, :])
+                eng.dma_start(t[r:P:32, :].bitcast(I32), src[0].bitcast(I32)[r:16:4, :])
 
         w1rows = w1.rearrange("(p j) c -> p j c", j=PACK)
 
@@ -80,16 +81,16 @@ def tile_picked_zcomp_sigmoid_po_kernel(tc, x_words, x_scales, e_words, e_scales
         offs_t = load_list("offs_t", offs)
         xw = load_words("xw", x_words)
         edges = [load_list("edge1_t", edge1), load_list("edge2_t", edge2)]
-        load_scale_rows(xs, x_scales)
+        load_scale_rows(xs, x_scales, nc.gpsimd)
         w1raw.append(load_w1(1))
         poss = [load_list("pos1_t", pos1), load_list("pos2_t", pos2)]
         w3w = load_words("w3w", w3_words)
         load_scale_rows(w3s, w3_scales)
 
-        def deal(name, src, dtype):
-            dst = new(name, [P, 512], dtype)
-            nc.gpsimd.tensor_copy(dst[:].rearrange("p (t c i) -> p c t i", t=PACK, i=4),
-                                  src[:].rearrange("p (c i t) -> p c t i", t=PACK, i=4))
+        def deal(name, src, dtype, t0, t1):
+            dst = new(name, [P, (t1 - t0) * P], dtype)
+            nc.gpsimd.tensor_copy(dst[:].rearrange("p (t c i) -> p c t i", t=t1 - t0, i=4),
+                                  src[:].rearrange("p (c i t) -> p c t i", t=PACK, i=4)[:, :, t0:t1, :])
             return dst
 
         egw = new("egw", [P, S], U32)
@@ -98,10 +99,10 @@ def tile_picked_zcomp_sigmoid_po_kernel(tc, x_words, x_scales, e_words, e_scales
         xgs = new("xgs", [P, S], U8)
         nc.vector.tensor_copy(egs[:], es[:].indirect(attr_t[:]))
         nc.vector.tensor_copy(egw[:], ew[:].indirect(attr_t[:]))
-        w2dw = deal("w2dw", w2w, U32)
-        w2ds = deal("w2ds", w2s, U8)
-        w3dw = deal("w3dw", w3w, U32)
-        w3ds = deal("w3ds", w3s, U8)
+        w2dw = deal("w2dw", w2w, U32, 0, PACK)
+        w2ds = [deal("w2ds%d" % u, w2s, U8, 2 * u, 2 * u + 2) for u in range(2)]
+        w3dw = deal("w3dw", w3w, U32, 0, PACK)
+        w3ds = deal("w3ds", w3s, U8, 0, PACK)
 
         w1b = new("w1b", [P, PACK, P, PACK], BF16)
 
@@ -110,8 +111,8 @@ def tile_picked_zcomp_sigmoid_po_kernel(tc, x_words, x_scales, e_words, e_scales
                                   w1raw[u][:].rearrange("p j (m t) -> p m j t", t=PACK))
 
         round_w1(0)
-        nc.vector.tensor_copy(xgw[:], xw[:].indirect(offs_t[:]))
         nc.vector.tensor_copy(xgs[:], xs[:].indirect(offs_t[:]))
+        nc.vector.tensor_copy(xgw[:], xw[:].indirect(offs_t[:]))
         round_w1(1)
 
         r_t = []
@@ -125,7 +126,7 @@ def tile_picked_zcomp_sigmoid_po_kernel(tc, x_words, x_scales, e_words, e_scales
         for t in range(PACK):
             bank = ps.tile([P, S], F32, name="rbank%d" % t, tag="r%d" % t)
             cols = slice(t * P, (t + 1) * P)
-            nc.tensor.matmul_mx(out=bank[:], lhsT=w2dw[:, cols].bitcast(FP8X4), lhsT_scale=w2ds[:, cols],
+            nc.tensor.matmul_mx(out=bank[:], lhsT=w2dw[:, cols].bitcast(FP8X4), lhsT_scale=w2ds[t // 2][:, t % 2 * P:(t % 2 + 1) * P],
                                 rhs=egw[:].bitcast(FP8X4), rhs_scale=egs[:], start=True, stop=True)
             rt = new("r%d" % t, [P, S], F32)
             nc.scalar.copy(rt[:], bank[:])

@@ -18,6 +18,7 @@ ALU = mybir.AluOpType
 P = 128
 PACK = 4
 HALF = V // 2
+W1_CUTS = (0, 256, 384, 512)
 
 
 def tile_picked_zcomp_sigmoid_po_kernel(tc, x_words, x_scales, e_words, e_scales, w1, w2_words, w2_scales, w3_words, w3_scales,
@@ -25,6 +26,7 @@ def tile_picked_zcomp_sigmoid_po_kernel(tc, x_words, x_scales, e_words, e_scales
     nc = tc.nc
     with ExitStack() as ctx:
         sb = ctx.enter_context(tc.tile_pool(name="sb", bufs=1))
+        shared = ctx.enter_context(tc.tile_pool(name="shared", bufs=1))
         ps = ctx.enter_context(tc.psum_pool(name="ps", bufs=1))
 
         def new(name, shape, dtype, tag=None):
@@ -61,34 +63,40 @@ def tile_picked_zcomp_sigmoid_po_kernel(tc, x_words, x_scales, e_words, e_scales
         for t in (w2s, w3s):
             nc.vector.memset(t[:].bitcast(I32), 0)
 
-        def load_scale_rows(t, src, eng=nc.sync):
-            for r in range(4):
+        def load_scale_rows(t, src, rows=range(4), eng=nc.sync):
+            for r in rows:
                 eng.dma_start(t[r:P:32, :].bitcast(I32), src[0].bitcast(I32)[r:16:4, :])
 
         w1rows = w1.rearrange("(p j) c -> p j c", j=PACK)
 
         def load_w1(u):
-            t = new("w1raw%d" % u, [P, PACK, H // 2], F32)
-            nc.sync.dma_start(t[:], w1rows[:, :, u * (H // 2):(u + 1) * (H // 2)])
+            c0, c1 = W1_CUTS[u], W1_CUTS[u + 1]
+            t = new("w1raw%d" % u, [P, PACK, c1 - c0], F32)
+            nc.sync.dma_start(t[:], w1rows[:, :, c0:c1])
             return t
 
+        load_scale_rows(xs, x_scales, (2, 3), nc.gpsimd)
         attr_t = load_list("attr_t", attr)
         es = load_scales("es", e_scales)
+        load_scale_rows(w2s, w2_scales, (0, 1))
         ew = load_words("ew", e_words)
         w2w = load_words("w2w", w2_words)
-        load_scale_rows(w2s, w2_scales)
-        w1raw = [load_w1(0)]
+        load_scale_rows(w2s, w2_scales, (2, 3))
+        load_scale_rows(xs, x_scales, (0, 1))
         offs_t = load_list("offs_t", offs)
         xw = load_words("xw", x_words)
+        w1raw = [load_w1(0)]
         edges = [load_list("edge1_t", edge1), load_list("edge2_t", edge2)]
-        load_scale_rows(xs, x_scales, nc.gpsimd)
-        w1raw.append(load_w1(1))
+        w1raw.extend([load_w1(1), load_w1(2)])
         poss = [load_list("pos1_t", pos1), load_list("pos2_t", pos2)]
         w3w = load_words("w3w", w3_words)
         load_scale_rows(w3s, w3_scales)
 
-        def deal(name, src, dtype, t0, t1):
-            dst = new(name, [P, (t1 - t0) * P], dtype)
+        def deal(name, src, dtype, t0, t1, tag=None, offset=None):
+            if offset is None:
+                dst = new(name, [P, (t1 - t0) * P], dtype, tag)
+            else:
+                dst = shared.tile([P, (t1 - t0) * P], dtype, name=name, offset=offset, align_bytes=64)
             nc.gpsimd.tensor_copy(dst[:].rearrange("p (t c i) -> p c t i", t=t1 - t0, i=4),
                                   src[:].rearrange("p (c i t) -> p c t i", t=PACK, i=4)[:, :, t0:t1, :])
             return dst
@@ -99,21 +107,18 @@ def tile_picked_zcomp_sigmoid_po_kernel(tc, x_words, x_scales, e_words, e_scales
         xgs = new("xgs", [P, S], U8)
         nc.vector.tensor_copy(egs[:], es[:].indirect(attr_t[:]))
         nc.vector.tensor_copy(egw[:], ew[:].indirect(attr_t[:]))
-        w2dw = deal("w2dw", w2w, U32, 0, PACK)
         w2ds = [deal("w2ds%d" % u, w2s, U8, 2 * u, 2 * u + 2) for u in range(2)]
-        w3dw = deal("w3dw", w3w, U32, 0, PACK)
-        w3ds = deal("w3ds", w3s, U8, 0, PACK)
 
-        w1b = new("w1b", [P, PACK, P, PACK], BF16)
+        w1b = shared.tile([P, PACK, P, PACK], BF16, name="w1b", offset=0, align_bytes=64)
 
         def round_w1(u):
-            nc.vector.tensor_copy(w1b[:, :, u * 64:(u + 1) * 64, :].rearrange("p t m j -> p m j t"),
+            nc.vector.tensor_copy(w1b[:, :, W1_CUTS[u] // PACK:W1_CUTS[u + 1] // PACK, :].rearrange("p t m j -> p m j t"),
                                   w1raw[u][:].rearrange("p j (m t) -> p m j t", t=PACK))
 
-        round_w1(0)
         nc.vector.tensor_copy(xgs[:], xs[:].indirect(offs_t[:]))
         nc.vector.tensor_copy(xgw[:], xw[:].indirect(offs_t[:]))
-        round_w1(1)
+        for u in range(3):
+            round_w1(u)
 
         r_t = []
         rg = {}
@@ -123,20 +128,25 @@ def tile_picked_zcomp_sigmoid_po_kernel(tc, x_words, x_scales, e_words, e_scales
             for d in range(2):
                 nc.scalar.activation(rg[t][:, d, :], r_t[t][:].indirect(edges[d][:]), ACT.Sigmoid)
 
-        for t in range(PACK):
-            bank = ps.tile([P, S], F32, name="rbank%d" % t, tag="r%d" % t)
-            cols = slice(t * P, (t + 1) * P)
-            nc.tensor.matmul_mx(out=bank[:], lhsT=w2dw[:, cols].bitcast(FP8X4), lhsT_scale=w2ds[t // 2][:, t % 2 * P:(t % 2 + 1) * P],
-                                rhs=egw[:].bitcast(FP8X4), rhs_scale=egs[:], start=True, stop=True)
-            rt = new("r%d" % t, [P, S], F32)
-            nc.scalar.copy(rt[:], bank[:])
-            r_t.append(rt)
+        rbanks = []
+        for u in range(2):
+            w2dw = deal("w2dw%d" % u, w2w, U32, 2 * u, 2 * u + 2, "w2dw")
+            for i in range(2):
+                t = 2 * u + i
+                bank = ps.tile([P, S], F32, name="rbank%d" % t, tag="r%d" % t)
+                cols = slice(i * P, (i + 1) * P)
+                nc.tensor.matmul_mx(out=bank[:], lhsT=w2dw[:, cols].bitcast(FP8X4), lhsT_scale=w2ds[u][:, cols],
+                                    rhs=egw[:].bitcast(FP8X4), rhs_scale=egs[:], start=True, stop=True)
+                rbanks.append(bank)
+        for t in range(PACK - 1):
+            r_t.append(new("r%d" % t, [P, S], F32, "r%d" % (t % 2)))
+            nc.scalar.copy(r_t[t][:], rbanks[t][:])
             if t < 2:
                 edge_gathers(t)
 
         hbanks = []
         for u in range(2):
-            w1w = new("w1w%d" % u, [P, 2 * P], U32)
+            w1w = new("w1w%d" % u, [P, 2 * P], U32, "w1w1" if u else "w2dw")
             w1s = new("w1s%d" % u, [P, 2 * P], U8)
             nc.vector.quantize_mx(out=w1w[:].bitcast(FP8X4), scales=w1s[:],
                                   in_=w1b[:, 2 * u:2 * u + 2, :, :].rearrange("p t m j -> p (t m j)"))
@@ -148,10 +158,14 @@ def tile_picked_zcomp_sigmoid_po_kernel(tc, x_words, x_scales, e_words, e_scales
                                     rhs=xgw[:].bitcast(FP8X4), rhs_scale=xgs[:], start=True, stop=True)
                 hbanks.append(bank)
 
+        w3dw = deal("w3dw", w3w, U32, 0, PACK, offset=0)
+        w3ds = deal("w3ds", w3s, U8, 0, PACK, offset=2048)
+        r_t.append(new("r3", [P, S], F32, "w1raw2"))
+        nc.vector.tensor_copy(r_t[3][:], rbanks[3][:])
         h_t = [new("h%d" % t, [P, S], F32) for t in range(PACK)]
         nc.vector.tensor_copy(h_t[0][:], hbanks[0][:])
         nc.scalar.copy(h_t[1][:], hbanks[1][:])
-        edge_gathers(2, "w1w0")
+        edge_gathers(2, "w2dw")
         nc.scalar.copy(h_t[2][:], hbanks[2][:])
         edge_gathers(3, "w1w1")
         nc.scalar.copy(h_t[3][:], hbanks[3][:])

@@ -26,7 +26,6 @@ def tile_picked_zcomp_sigmoid_po_kernel(tc, x_words, x_scales, e_words, e_scales
     nc = tc.nc
     with ExitStack() as ctx:
         sb = ctx.enter_context(tc.tile_pool(name="sb", bufs=1))
-        shared = ctx.enter_context(tc.tile_pool(name="shared", bufs=1))
         ps = ctx.enter_context(tc.psum_pool(name="ps", bufs=1))
 
         def new(name, shape, dtype, tag=None):
@@ -59,13 +58,12 @@ def tile_picked_zcomp_sigmoid_po_kernel(tc, x_words, x_scales, e_words, e_scales
         xs = new("xs", [P, T], U8)
         w2s = new("w2s", [P, H], U8)
         w3s = new("w3s", [P, N], U8)
-        nc.gpsimd.memset(xs[:].bitcast(I32), 0)
-        for t in (w2s, w3s):
+        for t in (w2s, xs, w3s):
             nc.vector.memset(t[:].bitcast(I32), 0)
 
-        def load_scale_rows(t, src, rows=range(4), eng=nc.sync):
-            for r in rows:
-                eng.dma_start(t[r:P:32, :].bitcast(I32), src[0].bitcast(I32)[r:16:4, :])
+        def load_scale_rows(t, src):
+            for r in range(4):
+                nc.sync.dma_start(t[r:P:32, :].bitcast(I32), src[0].bitcast(I32)[r:16:4, :])
 
         w1rows = w1.rearrange("(p j) c -> p j c", j=PACK)
 
@@ -75,30 +73,25 @@ def tile_picked_zcomp_sigmoid_po_kernel(tc, x_words, x_scales, e_words, e_scales
             nc.sync.dma_start(t[:], w1rows[:, :, c0:c1])
             return t
 
-        load_scale_rows(xs, x_scales, (2, 3), nc.gpsimd)
         attr_t = load_list("attr_t", attr)
         es = load_scales("es", e_scales)
-        load_scale_rows(w2s, w2_scales, (0, 1))
         ew = load_words("ew", e_words)
         w2w = load_words("w2w", w2_words)
-        load_scale_rows(w2s, w2_scales, (2, 3))
-        load_scale_rows(xs, x_scales, (0, 1))
-        offs_t = load_list("offs_t", offs)
+        load_scale_rows(w2s, w2_scales)
         xw = load_words("xw", x_words)
+        offs_t = load_list("offs_t", offs)
         w1raw = [load_w1(0)]
+        load_scale_rows(xs, x_scales)
         edges = [load_list("edge1_t", edge1), load_list("edge2_t", edge2)]
         w1raw.extend([load_w1(1), load_w1(2)])
         poss = [load_list("pos1_t", pos1), load_list("pos2_t", pos2)]
         w3w = load_words("w3w", w3_words)
         load_scale_rows(w3s, w3_scales)
 
-        def deal(name, src, dtype, t0, t1, tag=None, offset=None):
-            if offset is None:
-                dst = new(name, [P, (t1 - t0) * P], dtype, tag)
-            else:
-                dst = shared.tile([P, (t1 - t0) * P], dtype, name=name, offset=offset, align_bytes=64)
-            nc.gpsimd.tensor_copy(dst[:].rearrange("p (t c i) -> p c t i", t=t1 - t0, i=4),
-                                  src[:].rearrange("p (c i t) -> p c t i", t=PACK, i=4)[:, :, t0:t1, :])
+        def deal(name, src, dtype, tag=None):
+            dst = new(name, [P, 512], dtype, tag)
+            a, b = (dst[:], src[:]) if dtype == U8 else (dst[:].bitcast(I32), src[:].bitcast(I32))
+            nc.vector.tensor_copy(a.rearrange("p (t m) -> p m t", t=PACK), b.rearrange("p (m t) -> p m t", t=PACK))
             return dst
 
         egw = new("egw", [P, S], U32)
@@ -107,16 +100,17 @@ def tile_picked_zcomp_sigmoid_po_kernel(tc, x_words, x_scales, e_words, e_scales
         xgs = new("xgs", [P, S], U8)
         nc.vector.tensor_copy(egs[:], es[:].indirect(attr_t[:]))
         nc.vector.tensor_copy(egw[:], ew[:].indirect(attr_t[:]))
-        w2ds = [deal("w2ds%d" % u, w2s, U8, 2 * u, 2 * u + 2) for u in range(2)]
+        w2dw = deal("w2dw", w2w, U32)
+        w2ds = deal("w2ds", w2s, U8)
 
-        w1b = shared.tile([P, PACK, P, PACK], BF16, name="w1b", offset=0, align_bytes=64)
+        w1b = new("w1b", [P, PACK, P, PACK], BF16)
 
         def round_w1(u):
             nc.vector.tensor_copy(w1b[:, :, W1_CUTS[u] // PACK:W1_CUTS[u + 1] // PACK, :].rearrange("p t m j -> p m j t"),
                                   w1raw[u][:].rearrange("p j (m t) -> p m j t", t=PACK))
 
-        nc.vector.tensor_copy(xgs[:], xs[:].indirect(offs_t[:]))
         nc.vector.tensor_copy(xgw[:], xw[:].indirect(offs_t[:]))
+        nc.vector.tensor_copy(xgs[:], xs[:].indirect(offs_t[:]))
         for u in range(3):
             round_w1(u)
 
@@ -129,15 +123,12 @@ def tile_picked_zcomp_sigmoid_po_kernel(tc, x_words, x_scales, e_words, e_scales
                 nc.scalar.activation(rg[t][:, d, :], r_t[t][:].indirect(edges[d][:]), ACT.Sigmoid)
 
         rbanks = []
-        for u in range(2):
-            w2dw = deal("w2dw%d" % u, w2w, U32, 2 * u, 2 * u + 2, "w2dw")
-            for i in range(2):
-                t = 2 * u + i
-                bank = ps.tile([P, S], F32, name="rbank%d" % t, tag="r%d" % t)
-                cols = slice(i * P, (i + 1) * P)
-                nc.tensor.matmul_mx(out=bank[:], lhsT=w2dw[:, cols].bitcast(FP8X4), lhsT_scale=w2ds[u][:, cols],
-                                    rhs=egw[:].bitcast(FP8X4), rhs_scale=egs[:], start=True, stop=True)
-                rbanks.append(bank)
+        for t in range(PACK):
+            bank = ps.tile([P, S], F32, name="rbank%d" % t, tag="r%d" % t)
+            cols = slice(t * P, (t + 1) * P)
+            nc.tensor.matmul_mx(out=bank[:], lhsT=w2dw[:, cols].bitcast(FP8X4), lhsT_scale=w2ds[:, cols],
+                                rhs=egw[:].bitcast(FP8X4), rhs_scale=egs[:], start=True, stop=True)
+            rbanks.append(bank)
         for t in range(PACK - 1):
             r_t.append(new("r%d" % t, [P, S], F32, "r%d" % (t % 2)))
             nc.scalar.copy(r_t[t][:], rbanks[t][:])
@@ -158,10 +149,9 @@ def tile_picked_zcomp_sigmoid_po_kernel(tc, x_words, x_scales, e_words, e_scales
                                     rhs=xgw[:].bitcast(FP8X4), rhs_scale=xgs[:], start=True, stop=True)
                 hbanks.append(bank)
 
-        w3dw = deal("w3dw", w3w, U32, 0, PACK, offset=0)
-        w3ds = deal("w3ds", w3s, U8, 0, PACK, offset=2048)
         r_t.append(new("r3", [P, S], F32, "w1raw2"))
         nc.vector.tensor_copy(r_t[3][:], rbanks[3][:])
+        w3dw = deal("w3dw", w3w, U32, "w1b")
         h_t = [new("h%d" % t, [P, S], F32) for t in range(PACK)]
         nc.vector.tensor_copy(h_t[0][:], hbanks[0][:])
         nc.scalar.copy(h_t[1][:], hbanks[1][:])
@@ -180,6 +170,7 @@ def tile_picked_zcomp_sigmoid_po_kernel(tc, x_words, x_scales, e_words, e_scales
         for t in range(PACK - 1):
             node_gathers(t, 0, V)
 
+        w3ds = deal("w3ds", w3s, U8, "h1")
         ys = new("ys", [P, V], U8)
         yw = new("yw", [P, V], U32)
         out_rows = out_0.rearrange("(p t) v -> p t v", t=PACK)

@@ -26,6 +26,7 @@ def tile_picked_zcomp_sigmoid_po_kernel(tc, x_words, x_scales, e_words, e_scales
     nc = tc.nc
     with ExitStack() as ctx:
         sb = ctx.enter_context(tc.tile_pool(name="sb", bufs=1))
+        shared = ctx.enter_context(tc.tile_pool(name="shared", bufs=1))
         ps = ctx.enter_context(tc.psum_pool(name="ps", bufs=1))
 
         def new(name, shape, dtype, tag=None):
@@ -58,30 +59,34 @@ def tile_picked_zcomp_sigmoid_po_kernel(tc, x_words, x_scales, e_words, e_scales
         xs = new("xs", [P, T], U8)
         w2s = new("w2s", [P, H], U8)
         w3s = new("w3s", [P, N], U8)
-        for t in (w2s, xs, w3s):
+        nc.gpsimd.memset(xs[:].bitcast(I32), 0)
+        for t in (w2s, w3s):
             nc.vector.memset(t[:].bitcast(I32), 0)
 
-        def load_scale_rows(t, src):
+        def load_scale_rows(t, src, eng=nc.sync):
             for r in range(4):
-                nc.sync.dma_start(t[r:P:32, :].bitcast(I32), src[0].bitcast(I32)[r:16:4, :])
+                eng.dma_start(t[r:P:32, :].bitcast(I32), src[0].bitcast(I32)[r:16:4, :])
 
         w1rows = w1.rearrange("(p j) c -> p j c", j=PACK)
 
         def load_w1(u):
             c0, c1 = W1_CUTS[u], W1_CUTS[u + 1]
-            t = new("w1raw%d" % u, [P, PACK, c1 - c0], F32)
+            if u:
+                t = new("w1raw%d" % u, [P, PACK, c1 - c0], F32)
+            else:
+                t = shared.tile([P, PACK, c1 - c0], F32, name="w1raw0", offset=0, align_bytes=64)
             nc.sync.dma_start(t[:], w1rows[:, :, c0:c1])
             return t
 
+        load_scale_rows(xs, x_scales, nc.gpsimd)
         attr_t = load_list("attr_t", attr)
         es = load_scales("es", e_scales)
         ew = load_words("ew", e_words)
         w2w = load_words("w2w", w2_words)
         load_scale_rows(w2s, w2_scales)
-        xw = load_words("xw", x_words)
-        offs_t = load_list("offs_t", offs)
         w1raw = [load_w1(0)]
-        load_scale_rows(xs, x_scales)
+        offs_t = load_list("offs_t", offs)
+        xw = load_words("xw", x_words)
         edges = [load_list("edge1_t", edge1), load_list("edge2_t", edge2)]
         w1raw.extend([load_w1(1), load_w1(2)])
         poss = [load_list("pos1_t", pos1), load_list("pos2_t", pos2)]
@@ -96,7 +101,7 @@ def tile_picked_zcomp_sigmoid_po_kernel(tc, x_words, x_scales, e_words, e_scales
 
         egw = new("egw", [P, S], U32)
         egs = new("egs", [P, S], U8)
-        xgw = new("xgw", [P, S], U32)
+        xgw = new("xgw", [P, S], U32, "xs")
         xgs = new("xgs", [P, S], U8)
         nc.vector.tensor_copy(egs[:], es[:].indirect(attr_t[:]))
         nc.vector.tensor_copy(egw[:], ew[:].indirect(attr_t[:]))
@@ -106,21 +111,23 @@ def tile_picked_zcomp_sigmoid_po_kernel(tc, x_words, x_scales, e_words, e_scales
         w1b = new("w1b", [P, PACK, P, PACK], BF16)
 
         def round_w1(u):
-            nc.vector.tensor_copy(w1b[:, :, W1_CUTS[u] // PACK:W1_CUTS[u + 1] // PACK, :].rearrange("p t m j -> p m j t"),
-                                  w1raw[u][:].rearrange("p j (m t) -> p m j t", t=PACK))
+            copy = nc.vector.tensor_copy if u else nc.scalar.copy
+            copy(w1b[:, :, W1_CUTS[u] // PACK:W1_CUTS[u + 1] // PACK, :].rearrange("p t m j -> p m j t"),
+                 w1raw[u][:].rearrange("p j (m t) -> p m j t", t=PACK))
 
-        nc.vector.tensor_copy(xgw[:], xw[:].indirect(offs_t[:]))
         nc.vector.tensor_copy(xgs[:], xs[:].indirect(offs_t[:]))
+        nc.vector.tensor_copy(xgw[:], xw[:].indirect(offs_t[:]))
         for u in range(3):
             round_w1(u)
 
         r_t = []
         rg = {}
 
-        def edge_gathers(t, tag=None):
+        def edge_gathers(t, tag=None, n=V):
             rg[t] = new("rg%d" % t, [P, 2, V], F32, tag)
-            for d in range(2):
-                nc.scalar.activation(rg[t][:, d, :], r_t[t][:].indirect(edges[d][:]), ACT.Sigmoid)
+            for v0 in range(0, V, n):
+                for d in range(2):
+                    nc.scalar.activation(rg[t][:, d, v0:v0 + n], r_t[t][:].indirect(edges[d][:, v0 // 16:(v0 + n) // 16]), ACT.Sigmoid)
 
         rbanks = []
         for t in range(PACK):
@@ -130,7 +137,7 @@ def tile_picked_zcomp_sigmoid_po_kernel(tc, x_words, x_scales, e_words, e_scales
                                 rhs=egw[:].bitcast(FP8X4), rhs_scale=egs[:], start=True, stop=True)
             rbanks.append(bank)
         for t in range(PACK - 1):
-            r_t.append(new("r%d" % t, [P, S], F32, "r%d" % (t % 2)))
+            r_t.append(shared.tile([P, S], F32, name="r%d" % t, offset=t % 2 * S * 4, align_bytes=64))
             nc.scalar.copy(r_t[t][:], rbanks[t][:])
             if t < 2:
                 edge_gathers(t)
@@ -157,8 +164,8 @@ def tile_picked_zcomp_sigmoid_po_kernel(tc, x_words, x_scales, e_words, e_scales
         nc.scalar.copy(h_t[1][:], hbanks[1][:])
         edge_gathers(2, "w2dw")
         nc.scalar.copy(h_t[2][:], hbanks[2][:])
-        edge_gathers(3, "w1w1")
         nc.scalar.copy(h_t[3][:], hbanks[3][:])
+        edge_gathers(3, "w1w1", HALF)
 
         prod = [new("prod%d" % d, [P, PACK, V], F32) for d in range(2)]
 

@@ -18,7 +18,7 @@ ALU = mybir.AluOpType
 P = 128
 PACK = 4
 HALF = V // 2
-W1_CUTS = (0, 256, 384, 512)
+W1_CUTS = (0, 128, 384, 512)
 
 
 def tile_picked_zcomp_sigmoid_po_kernel(tc, x_words, x_scales, e_words, e_scales, w1, w2_words, w2_scales, w3_words, w3_scales,
@@ -59,13 +59,12 @@ def tile_picked_zcomp_sigmoid_po_kernel(tc, x_words, x_scales, e_words, e_scales
         xs = new("xs", [P, T], U8)
         w2s = new("w2s", [P, H], U8)
         w3s = new("w3s", [P, N], U8)
-        nc.gpsimd.memset(xs[:].bitcast(I32), 0)
-        for t in (w2s, w3s):
+        for t in (w2s, xs, w3s):
             nc.vector.memset(t[:].bitcast(I32), 0)
 
-        def load_scale_rows(t, src, eng=nc.sync):
+        def load_scale_rows(t, src):
             for r in range(4):
-                eng.dma_start(t[r:P:32, :].bitcast(I32), src[0].bitcast(I32)[r:16:4, :])
+                nc.sync.dma_start(t[r:P:32, :].bitcast(I32), src[0].bitcast(I32)[r:16:4, :])
 
         w1rows = w1.rearrange("(p j) c -> p j c", j=PACK)
 
@@ -74,21 +73,22 @@ def tile_picked_zcomp_sigmoid_po_kernel(tc, x_words, x_scales, e_words, e_scales
             if u:
                 t = new("w1raw%d" % u, [P, PACK, c1 - c0], F32)
             else:
-                t = shared.tile([P, PACK, c1 - c0], F32, name="w1raw0", offset=0, align_bytes=64)
+                t = shared.tile([P, PACK, c1 - c0], F32, name="w1raw0", offset=S * 2, align_bytes=64)
             nc.sync.dma_start(t[:], w1rows[:, :, c0:c1])
             return t
 
-        load_scale_rows(xs, x_scales, nc.gpsimd)
         attr_t = load_list("attr_t", attr)
         es = load_scales("es", e_scales)
         ew = load_words("ew", e_words)
         w2w = load_words("w2w", w2_words)
-        load_scale_rows(w2s, w2_scales)
-        w1raw = [load_w1(0)]
         offs_t = load_list("offs_t", offs)
+        load_scale_rows(w2s, w2_scales)
         xw = load_words("xw", x_words)
+        w1raw = [load_w1(0)]
+        load_scale_rows(xs, x_scales)
+        w1raw.append(load_w1(1))
         edges = [load_list("edge1_t", edge1), load_list("edge2_t", edge2)]
-        w1raw.extend([load_w1(1), load_w1(2)])
+        w1raw.append(load_w1(2))
         poss = [load_list("pos1_t", pos1), load_list("pos2_t", pos2)]
         w3w = load_words("w3w", w3_words)
         load_scale_rows(w3s, w3_scales)
@@ -101,7 +101,7 @@ def tile_picked_zcomp_sigmoid_po_kernel(tc, x_words, x_scales, e_words, e_scales
 
         egw = new("egw", [P, S], U32)
         egs = new("egs", [P, S], U8)
-        xgw = new("xgw", [P, S], U32, "xs")
+        xgw = new("xgw", [P, S], U32)
         xgs = new("xgs", [P, S], U8)
         nc.vector.tensor_copy(egs[:], es[:].indirect(attr_t[:]))
         nc.vector.tensor_copy(egw[:], ew[:].indirect(attr_t[:]))
@@ -115,8 +115,8 @@ def tile_picked_zcomp_sigmoid_po_kernel(tc, x_words, x_scales, e_words, e_scales
             copy(w1b[:, :, W1_CUTS[u] // PACK:W1_CUTS[u + 1] // PACK, :].rearrange("p t m j -> p m j t"),
                  w1raw[u][:].rearrange("p j (m t) -> p m j t", t=PACK))
 
-        nc.vector.tensor_copy(xgs[:], xs[:].indirect(offs_t[:]))
         nc.vector.tensor_copy(xgw[:], xw[:].indirect(offs_t[:]))
+        nc.vector.tensor_copy(xgs[:], xs[:].indirect(offs_t[:]))
         for u in range(3):
             round_w1(u)
 

@@ -136,7 +136,7 @@ def tile_picked_zcomp_sigmoid_po_kernel(tc, x_words, x_scales, e_words, e_scales
             nc.tensor.matmul_mx(out=bank[:], lhsT=w2dw[:, cols].bitcast(FP8X4), lhsT_scale=w2ds[:, cols],
                                 rhs=egw[:].bitcast(FP8X4), rhs_scale=egs[:], start=True, stop=True)
             rbanks.append(bank)
-        for t in range(PACK - 1):
+        for t in range(PACK):
             r_t.append(shared.tile([P, S], F32, name="r%d" % t, offset=t % 2 * S * 4, align_bytes=64))
             nc.scalar.copy(r_t[t][:], rbanks[t][:])
             if t < 2:
@@ -156,8 +156,6 @@ def tile_picked_zcomp_sigmoid_po_kernel(tc, x_words, x_scales, e_words, e_scales
                                     rhs=xgw[:].bitcast(FP8X4), rhs_scale=xgs[:], start=True, stop=True)
                 hbanks.append(bank)
 
-        r_t.append(new("r3", [P, S], F32, "w1raw2"))
-        nc.vector.tensor_copy(r_t[3][:], rbanks[3][:])
         w3dw = deal("w3dw", w3w, U32, "w1b")
         h_t = [new("h%d" % t, [P, S], F32) for t in range(PACK)]
         nc.vector.tensor_copy(h_t[0][:], hbanks[0][:])

@@ -77,6 +77,7 @@ def tile_picked_zcomp_sigmoid_po_kernel(tc, x_words, x_scales, e_words, e_scales
             nc.sync.dma_start(t[:], w1rows[:, :, c0:c1])
             return t
 
+        nc.gpsimd.dma_start(w2s[4:P:8, :].bitcast(I32), w3_scales[0].bitcast(I32))
         attr_t = load_list("attr_t", attr)
         es = load_scales("es", e_scales)
         ew = load_words("ew", e_words)
@@ -91,7 +92,6 @@ def tile_picked_zcomp_sigmoid_po_kernel(tc, x_words, x_scales, e_words, e_scales
         w1raw.append(load_w1(2))
         poss = [load_list("pos1_t", pos1), load_list("pos2_t", pos2)]
         w3w = load_words("w3w", w3_words)
-        load_scale_rows(w3s, w3_scales)
 
         def deal(name, src, dtype, tag=None):
             dst = new(name, [P, 512], dtype, tag)
@@ -107,6 +107,8 @@ def tile_picked_zcomp_sigmoid_po_kernel(tc, x_words, x_scales, e_words, e_scales
         nc.vector.tensor_copy(egw[:], ew[:].indirect(attr_t[:]))
         w2dw = deal("w2dw", w2w, U32)
         w2ds = deal("w2ds", w2s, U8)
+        for r in range(4):
+            nc.sync.dma_start(w3s[r:P:32, :].bitcast(I32), w2ds[8 * r + 4:P:32, :].bitcast(I32))
 
         w1b = new("w1b", [P, PACK, P, PACK], BF16)
 
@@ -175,7 +177,6 @@ def tile_picked_zcomp_sigmoid_po_kernel(tc, x_words, x_scales, e_words, e_scales
         for t in range(PACK - 1):
             node_gathers(t, 0, V)
 
-        w3ds = deal("w3ds", w3s, U8, "h1")
         ys = new("ys", [P, V], U8)
         yw = new("yw", [P, V], U32)
         out_rows = out_0.rearrange("(p t) v -> p t v", t=PACK)
@@ -202,7 +203,7 @@ def tile_picked_zcomp_sigmoid_po_kernel(tc, x_words, x_scales, e_words, e_scales
             banks = [ps.tile([P, per, HALF], F32, name="ybank%d_%d" % (a, k), tag="r%d" % (a + k)) for k in range(nb)]
             for t in range(PACK):
                 cols = slice(t * P, (t + 1) * P)
-                nc.tensor.matmul_mx(out=banks[t // per][:, t % per, :], lhsT=w3dw[:, cols].bitcast(FP8X4), lhsT_scale=w3ds[:, cols],
+                nc.tensor.matmul_mx(out=banks[t // per][:, t % per, :], lhsT=w3dw[:, cols].bitcast(FP8X4), lhsT_scale=w3s[:, cols],
                                     rhs=zw[:].bitcast(FP8X4), rhs_scale=zs[:], start=True, stop=True)
             if a == 0:
                 nc.scalar.copy(yb[:].rearrange("p (c i) t -> p c t i", i=2),

@@ -58,12 +58,11 @@ def tile_picked_zcomp_sigmoid_po_kernel(tc, x_words, x_scales, e_words, e_scales
 
         xs = new("xs", [P, T], U8)
         w2s = new("w2s", [P, H], U8)
-        w3s = new("w3s", [P, N], U8)
-        for t in (w2s, xs, w3s):
+        for t in (w2s, xs):
             nc.vector.memset(t[:].bitcast(I32), 0)
 
-        def load_scale_rows(t, src):
-            for r in range(4):
+        def load_scale_rows(t, src, rows=range(4)):
+            for r in rows:
                 nc.sync.dma_start(t[r:P:32, :].bitcast(I32), src[0].bitcast(I32)[r:16:4, :])
 
         w1rows = w1.rearrange("(p j) c -> p j c", j=PACK)
@@ -77,13 +76,14 @@ def tile_picked_zcomp_sigmoid_po_kernel(tc, x_words, x_scales, e_words, e_scales
             nc.sync.dma_start(t[:], w1rows[:, :, c0:c1])
             return t
 
-        nc.gpsimd.dma_start(w2s[4:P:8, :].bitcast(I32), w3_scales[0].bitcast(I32))
         attr_t = load_list("attr_t", attr)
         es = load_scales("es", e_scales)
+        load_scale_rows(w2s, w2_scales, range(1))
         ew = load_words("ew", e_words)
         w2w = load_words("w2w", w2_words)
+        load_scale_rows(w2s, w2_scales, range(1, 4))
+        nc.sync.dma_start(w2s[4:P:8, :].bitcast(I32), w3_scales[0].bitcast(I32))
         offs_t = load_list("offs_t", offs)
-        load_scale_rows(w2s, w2_scales)
         xw = load_words("xw", x_words)
         w1raw = [load_w1(0)]
         load_scale_rows(xs, x_scales)
@@ -107,8 +107,6 @@ def tile_picked_zcomp_sigmoid_po_kernel(tc, x_words, x_scales, e_words, e_scales
         nc.vector.tensor_copy(egw[:], ew[:].indirect(attr_t[:]))
         w2dw = deal("w2dw", w2w, U32)
         w2ds = deal("w2ds", w2s, U8)
-        for r in range(4):
-            nc.sync.dma_start(w3s[r:P:32, :].bitcast(I32), w2ds[8 * r + 4:P:32, :].bitcast(I32))
 
         w1b = new("w1b", [P, PACK, P, PACK], BF16)
 
@@ -145,10 +143,14 @@ def tile_picked_zcomp_sigmoid_po_kernel(tc, x_words, x_scales, e_words, e_scales
                 edge_gathers(t)
 
         hbanks = []
+        w13s = new("w13s", [P, H], U8)
         for u in range(2):
-            w1w = new("w1w%d" % u, [P, 2 * P], U32, "w1w1" if u else "w2dw")
-            w1s = new("w1s%d" % u, [P, 2 * P], U8)
-            nc.vector.quantize_mx(out=w1w[:].bitcast(FP8X4), scales=w1s[:],
+            if u:
+                w1w = shared.tile([P, 2 * P], U32, name="w1w1", offset=(2 * S + HALF) * 4, align_bytes=64)
+            else:
+                w1w = new("w1w0", [P, 2 * P], U32, "w2dw")
+            w1s = w13s[:, 2 * P * u:2 * P * (u + 1)]
+            nc.vector.quantize_mx(out=w1w[:].bitcast(FP8X4), scales=w1s,
                                   in_=w1b[:, 2 * u:2 * u + 2, :, :].rearrange("p t m j -> p (t m j)"))
             for i in range(2):
                 t = 2 * u + i
@@ -158,6 +160,8 @@ def tile_picked_zcomp_sigmoid_po_kernel(tc, x_words, x_scales, e_words, e_scales
                                     rhs=xgw[:].bitcast(FP8X4), rhs_scale=xgs[:], start=True, stop=True)
                 hbanks.append(bank)
 
+        for r in range(4):
+            nc.sync.dma_start(w13s[4 + r:P:32, :].bitcast(I32), w2ds[8 * r + 4:P:32, :].bitcast(I32))
         w3dw = deal("w3dw", w3w, U32, "w1b")
         h_t = [new("h%d" % t, [P, S], F32) for t in range(PACK)]
         nc.vector.tensor_copy(h_t[0][:], hbanks[0][:])
@@ -165,7 +169,16 @@ def tile_picked_zcomp_sigmoid_po_kernel(tc, x_words, x_scales, e_words, e_scales
         edge_gathers(2, "w2dw")
         nc.scalar.copy(h_t[2][:], hbanks[2][:])
         nc.scalar.copy(h_t[3][:], hbanks[3][:])
-        edge_gathers(3, "w1w1", HALF)
+        mid = shared.tile([P, 2, HALF], F32, name="rg3mid", offset=2 * S * 4, align_bytes=64)
+        ends = [shared.tile([P, HALF], F32, name="rg3end%d" % a, offset=(2 * S + V) * 4, align_bytes=64) for a in range(2)]
+        rg3 = {(0, 0): ends[0][:], (0, 1): mid[:, 0, :], (1, 0): mid[:, 1, :], (1, 1): ends[1][:]}
+
+        def last_edge_gather(a, d):
+            nc.scalar.activation(rg3[a, d], r_t[3][:].indirect(edges[d][:, a * HALF // 16:(a + 1) * HALF // 16]), ACT.Sigmoid)
+
+        last_edge_gather(0, 0)
+        last_edge_gather(0, 1)
+        last_edge_gather(1, 0)
 
         prod = [new("prod%d" % d, [P, PACK, V], F32) for d in range(2)]
 
@@ -184,7 +197,11 @@ def tile_picked_zcomp_sigmoid_po_kernel(tc, x_words, x_scales, e_words, e_scales
         zq = []
         for a in range(2):
             v0 = a * HALF
-            node_gathers(PACK - 1, v0, HALF)
+            for d in range(2):
+                nc.vector.tensor_tensor(prod[d][:, 3, v0:v0 + HALF], h_t[3][:].indirect(poss[d][:, v0 // 16:(v0 + HALF) // 16]),
+                                        rg3[a, d], ALU.mult)
+                if a == 0 and d == 0:
+                    last_edge_gather(1, 1)
             zb = new("zb%d" % a, [P, HALF, PACK], BF16)
             nc.vector.tensor_tensor(zb[:].rearrange("p (c i) t -> p c t i", i=2),
                                     prod[0][:, :, v0:v0 + HALF].rearrange("p t (c i) -> p c t i", i=2),
@@ -203,13 +220,13 @@ def tile_picked_zcomp_sigmoid_po_kernel(tc, x_words, x_scales, e_words, e_scales
             banks = [ps.tile([P, per, HALF], F32, name="ybank%d_%d" % (a, k), tag="r%d" % (a + k)) for k in range(nb)]
             for t in range(PACK):
                 cols = slice(t * P, (t + 1) * P)
-                nc.tensor.matmul_mx(out=banks[t // per][:, t % per, :], lhsT=w3dw[:, cols].bitcast(FP8X4), lhsT_scale=w3s[:, cols],
+                nc.tensor.matmul_mx(out=banks[t // per][:, t % per, :], lhsT=w3dw[:, cols].bitcast(FP8X4), lhsT_scale=w13s[4:P, cols],
                                     rhs=zw[:].bitcast(FP8X4), rhs_scale=zs[:], start=True, stop=True)
             if a == 0:
-                nc.scalar.copy(yb[:].rearrange("p (c i) t -> p c t i", i=2),
-                               banks[0][:].rearrange("p t (c i) -> p c t i", i=2))
                 nc.scalar.copy(y[:], banks[0][:])
                 nc.sync.dma_start(out_rows[:, :, v0:v0 + HALF], y[:])
+                nc.scalar.copy(yb[:].rearrange("p (c i) t -> p c t i", i=2),
+                               banks[0][:].rearrange("p t (c i) -> p c t i", i=2))
             else:
                 for k in range(nb):
                     rows = slice(k * per, (k + 1) * per)

@@ -69,10 +69,7 @@ def tile_picked_zcomp_sigmoid_po_kernel(tc, x_words, x_scales, e_words, e_scales
 
         def load_w1(u):
             c0, c1 = W1_CUTS[u], W1_CUTS[u + 1]
-            if u:
-                t = new("w1raw%d" % u, [P, PACK, c1 - c0], F32)
-            else:
-                t = shared.tile([P, PACK, c1 - c0], F32, name="w1raw0", offset=S * 2, align_bytes=64)
+            t = new("w1raw%d" % u, [P, PACK, c1 - c0], F32)
             nc.sync.dma_start(t[:], w1rows[:, :, c0:c1])
             return t
 
@@ -90,8 +87,8 @@ def tile_picked_zcomp_sigmoid_po_kernel(tc, x_words, x_scales, e_words, e_scales
         w1raw.append(load_w1(1))
         edges = [load_list("edge1_t", edge1), load_list("edge2_t", edge2)]
         w1raw.append(load_w1(2))
-        poss = [load_list("pos1_t", pos1), load_list("pos2_t", pos2)]
         w3w = load_words("w3w", w3_words)
+        poss = [load_list("pos1_t", pos1), load_list("pos2_t", pos2)]
 
         def deal(name, src, dtype, tag=None):
             dst = new(name, [P, 512], dtype, tag)
@@ -110,15 +107,16 @@ def tile_picked_zcomp_sigmoid_po_kernel(tc, x_words, x_scales, e_words, e_scales
 
         w1b = new("w1b", [P, PACK, P, PACK], BF16)
 
-        def round_w1(u):
-            copy = nc.vector.tensor_copy if u else nc.scalar.copy
-            copy(w1b[:, :, W1_CUTS[u] // PACK:W1_CUTS[u + 1] // PACK, :].rearrange("p t m j -> p m j t"),
-                 w1raw[u][:].rearrange("p j (m t) -> p m j t", t=PACK))
+        def round_w1(u, t0=0, t1=PACK):
+            nc.vector.tensor_copy(w1b[:, t0:t1, W1_CUTS[u] // PACK:W1_CUTS[u + 1] // PACK, :].rearrange("p t m j -> p m j t"),
+                 w1raw[u][:].rearrange("p j (m t) -> p m j t", t=PACK)[:, :, :, t0:t1])
 
         nc.vector.tensor_copy(xgw[:], xw[:].indirect(offs_t[:]))
         nc.vector.tensor_copy(xgs[:], xs[:].indirect(offs_t[:]))
-        for u in range(3):
-            round_w1(u)
+        round_w1(0)
+        round_w1(1)
+        round_w1(2, 0, 2)
+        round_w1(2, 2, PACK)
 
         r_t = []
         rg = {}
@@ -137,10 +135,10 @@ def tile_picked_zcomp_sigmoid_po_kernel(tc, x_words, x_scales, e_words, e_scales
                                 rhs=egw[:].bitcast(FP8X4), rhs_scale=egs[:], start=True, stop=True)
             rbanks.append(bank)
         for t in range(PACK):
-            r_t.append(shared.tile([P, S], F32, name="r%d" % t, offset=t % 2 * S * 4, align_bytes=64))
+            r_t.append(new("r%d" % t, [P, S], F32))
             nc.scalar.copy(r_t[t][:], rbanks[t][:])
-            if t < 2:
-                edge_gathers(t)
+        edge_gathers(0)
+        edge_gathers(1)
 
         hbanks = []
         w13s = new("w13s", [P, H], U8)

@@ -84,8 +84,9 @@ def tile_picked_zcomp_sigmoid_po_kernel(tc, x_words, x_scales, e_words, e_scales
         xw = load_words("xw", x_words)
         w1raw = [load_w1(0)]
         load_scale_rows(xs, x_scales)
+        edges = [load_list("edge1_t", edge1)]
         w1raw.append(load_w1(1))
-        edges = [load_list("edge1_t", edge1), load_list("edge2_t", edge2)]
+        edges.append(load_list("edge2_t", edge2))
         w1raw.append(load_w1(2))
         w3w = load_words("w3w", w3_words)
         poss = [load_list("pos1_t", pos1), load_list("pos2_t", pos2)]
@@ -103,7 +104,10 @@ def tile_picked_zcomp_sigmoid_po_kernel(tc, x_words, x_scales, e_words, e_scales
         nc.vector.tensor_copy(egs[:], es[:].indirect(attr_t[:]))
         nc.vector.tensor_copy(egw[:], ew[:].indirect(attr_t[:]))
         w2dw = deal("w2dw", w2w, U32)
-        w2ds = deal("w2ds", w2s, U8)
+        w2ds = new("w2ds", [P, H], U8)
+        for t0, t1 in ((0, 1), (1, PACK)):
+            nc.vector.tensor_copy(w2ds[:].rearrange("p (t m) -> p m t", t=PACK)[:, :, t0:t1],
+                                  w2s[:].rearrange("p (m t) -> p m t", t=PACK)[:, :, t0:t1])
 
         w1b = new("w1b", [P, PACK, P, PACK], BF16)
 
@@ -121,11 +125,9 @@ def tile_picked_zcomp_sigmoid_po_kernel(tc, x_words, x_scales, e_words, e_scales
         r_t = []
         rg = {}
 
-        def edge_gathers(t, tag=None, n=V):
-            rg[t] = new("rg%d" % t, [P, 2, V], F32, tag)
-            for v0 in range(0, V, n):
-                for d in range(2):
-                    nc.scalar.activation(rg[t][:, d, v0:v0 + n], r_t[t][:].indirect(edges[d][:, v0 // 16:(v0 + n) // 16]), ACT.Sigmoid)
+        def edge_gather(t, d, tag=None):
+            rg[t, d] = new("rg%d_%d" % (t, d), [P, V], F32, tag)
+            nc.scalar.activation(rg[t, d][:], r_t[t][:].indirect(edges[d][:]), ACT.Sigmoid)
 
         rbanks = []
         for t in range(PACK):
@@ -137,34 +139,42 @@ def tile_picked_zcomp_sigmoid_po_kernel(tc, x_words, x_scales, e_words, e_scales
         for t in range(PACK):
             r_t.append(new("r%d" % t, [P, S], F32))
             nc.scalar.copy(r_t[t][:], rbanks[t][:])
-        edge_gathers(0)
-        edge_gathers(1)
+        for t in range(PACK - 1):
+            edge_gather(t, 0)
+        for t in range(2):
+            edge_gather(t, 1)
 
         hbanks = []
         w13s = new("w13s", [P, H], U8)
-        for u in range(2):
-            if u:
-                w1w = shared.tile([P, 2 * P], U32, name="w1w1", offset=(2 * S + HALF) * 4, align_bytes=64)
+
+        def h_product(bank, w1w, t, t0, j0, j1):
+            nc.tensor.matmul_mx(out=bank[:], lhsT=w1w[:, (t - t0) * P:(t - t0 + 1) * P].bitcast(FP8X4), lhsT_scale=w13s[:, t * P:(t + 1) * P],
+                                rhs=xgw[:, j0:j1].bitcast(FP8X4), rhs_scale=xgs[:, j0:j1], start=True, stop=True)
+
+        for t0, t1 in ((0, 1), (1, 2), (2, PACK)):
+            if t0 == 2:
+                w1w = shared.tile([P, 2 * P], U32, name="w1w2", offset=(2 * S + HALF) * 4, align_bytes=64)
             else:
-                w1w = new("w1w0", [P, 2 * P], U32, "w2dw")
-            w1s = w13s[:, 2 * P * u:2 * P * (u + 1)]
-            nc.vector.quantize_mx(out=w1w[:].bitcast(FP8X4), scales=w1s,
-                                  in_=w1b[:, 2 * u:2 * u + 2, :, :].rearrange("p t m j -> p (t m j)"))
-            for i in range(2):
-                t = 2 * u + i
-                bank = ps.tile([P, S], F32, name="hbank%d" % t, tag="h%d" % t)
-                cols = slice(i * P, (i + 1) * P)
-                nc.tensor.matmul_mx(out=bank[:], lhsT=w1w[:, cols].bitcast(FP8X4), lhsT_scale=w1s[:, cols],
-                                    rhs=xgw[:].bitcast(FP8X4), rhs_scale=xgs[:], start=True, stop=True)
-                hbanks.append(bank)
+                w1w = new("w1w%d" % t0, [P, P], U32, "w2dw" if t0 else None)
+            nc.vector.quantize_mx(out=w1w[:].bitcast(FP8X4), scales=w13s[:, P * t0:P * t1],
+                                  in_=w1b[:, t0:t1, :, :].rearrange("p t m j -> p (t m j)"))
+            for t in range(t0, t1):
+                if t:
+                    hbanks.append(ps.tile([P, S], F32, name="hbank%d" % t, tag="h%d" % t))
+                    h_product(hbanks[t], w1w, t, t0, 0, S)
+                else:
+                    hbanks.append([ps.tile([P, S // 2], F32, name="hbank0_%d" % a, tag=("h0", "r0")[a]) for a in range(2)])
+                    for a in range(2):
+                        h_product(hbanks[0][a], w1w, t, t0, a * S // 2, (a + 1) * S // 2)
 
         for r in range(4):
             nc.sync.dma_start(w13s[4 + r:P:32, :].bitcast(I32), w2ds[8 * r + 4:P:32, :].bitcast(I32))
-        w3dw = deal("w3dw", w3w, U32, "w1b")
+        w3dw = deal("w3dw", w3w, U32)
         h_t = [new("h%d" % t, [P, S], F32) for t in range(PACK)]
-        nc.vector.tensor_copy(h_t[0][:], hbanks[0][:])
+        for a in range(2):
+            nc.vector.tensor_copy(h_t[0][:, a * S // 2:(a + 1) * S // 2], hbanks[0][a][:])
         nc.scalar.copy(h_t[1][:], hbanks[1][:])
-        edge_gathers(2, "w2dw")
+        edge_gather(2, 1, "w2dw")
         nc.scalar.copy(h_t[2][:], hbanks[2][:])
         nc.scalar.copy(h_t[3][:], hbanks[3][:])
         mid = shared.tile([P, 2, HALF], F32, name="rg3mid", offset=2 * S * 4, align_bytes=64)
@@ -183,7 +193,7 @@ def tile_picked_zcomp_sigmoid_po_kernel(tc, x_words, x_scales, e_words, e_scales
         def node_gathers(t, v0, n):
             for d in range(2):
                 nc.vector.tensor_tensor(prod[d][:, t, v0:v0 + n], h_t[t][:].indirect(poss[d][:, v0 // 16:(v0 + n) // 16]),
-                                        rg[t][:, d, v0:v0 + n], ALU.mult)
+                                        rg[t, d][:, v0:v0 + n], ALU.mult)
 
         for t in range(PACK - 1):
             node_gathers(t, 0, V)

@@ -86,10 +86,10 @@ def tile_picked_zcomp_sigmoid_po_kernel(tc, x_words, x_scales, e_words, e_scales
         load_scale_rows(xs, x_scales)
         edges = [load_list("edge1_t", edge1)]
         w1raw.append(load_w1(1))
-        edges.append(load_list("edge2_t", edge2))
         w1raw.append(load_w1(2))
         w3w = load_words("w3w", w3_words)
         poss = [load_list("pos1_t", pos1), load_list("pos2_t", pos2)]
+        edges.append(load_list("edge2_t", edge2))
 
         def deal(name, src, dtype, tag=None):
             dst = new(name, [P, 512], dtype, tag)
@@ -137,7 +137,7 @@ def tile_picked_zcomp_sigmoid_po_kernel(tc, x_words, x_scales, e_words, e_scales
                                 rhs=egw[:].bitcast(FP8X4), rhs_scale=egs[:], start=True, stop=True)
             rbanks.append(bank)
         for t in range(PACK):
-            r_t.append(new("r%d" % t, [P, S], F32))
+            r_t.append(shared.tile([P, S], F32, name="r1", offset=S * 4, align_bytes=64) if t == 1 else new("r%d" % t, [P, S], F32))
             nc.scalar.copy(r_t[t][:], rbanks[t][:])
         for t in range(PACK - 1):
             edge_gather(t, 0)
@@ -152,33 +152,32 @@ def tile_picked_zcomp_sigmoid_po_kernel(tc, x_words, x_scales, e_words, e_scales
                                 rhs=xgw[:, j0:j1].bitcast(FP8X4), rhs_scale=xgs[:, j0:j1], start=True, stop=True)
 
         for t0, t1 in ((0, 1), (1, 2), (2, PACK)):
-            if t0 == 2:
-                w1w = shared.tile([P, 2 * P], U32, name="w1w2", offset=(2 * S + HALF) * 4, align_bytes=64)
-            else:
-                w1w = new("w1w%d" % t0, [P, P], U32, "w2dw" if t0 else None)
+            w1w = new("w1w%d" % t0, [P, (t1 - t0) * P], U32, "w2dw" if t0 == 1 else None)
             nc.vector.quantize_mx(out=w1w[:].bitcast(FP8X4), scales=w13s[:, P * t0:P * t1],
                                   in_=w1b[:, t0:t1, :, :].rearrange("p t m j -> p (t m j)"))
             for t in range(t0, t1):
-                if t:
+                if t > 1:
                     hbanks.append(ps.tile([P, S], F32, name="hbank%d" % t, tag="h%d" % t))
                     h_product(hbanks[t], w1w, t, t0, 0, S)
                 else:
-                    hbanks.append([ps.tile([P, S // 2], F32, name="hbank0_%d" % a, tag=("h0", "r0")[a]) for a in range(2)])
+                    hbanks.append([ps.tile([P, S // 2], F32, name="hbank%d_%d" % (t, a), tag="%s%d" % ("hr"[a], t)) for a in range(2)])
                     for a in range(2):
-                        h_product(hbanks[0][a], w1w, t, t0, a * S // 2, (a + 1) * S // 2)
+                        h_product(hbanks[t][a], w1w, t, t0, a * S // 2, (a + 1) * S // 2)
 
         for r in range(4):
             nc.sync.dma_start(w13s[4 + r:P:32, :].bitcast(I32), w2ds[8 * r + 4:P:32, :].bitcast(I32))
         w3dw = deal("w3dw", w3w, U32)
-        h_t = [new("h%d" % t, [P, S], F32) for t in range(PACK)]
+        h_t = [new("h0", [P, S], F32), new("h1", [P, S], F32, "r0"),
+               shared.tile([P, S], F32, name="h2", offset=64, align_bytes=64), new("h3", [P, S], F32, "r2")]
         for a in range(2):
             nc.vector.tensor_copy(h_t[0][:, a * S // 2:(a + 1) * S // 2], hbanks[0][a][:])
-        nc.scalar.copy(h_t[1][:], hbanks[1][:])
+        nc.vector.tensor_copy(h_t[1][:, 0:S // 2], hbanks[1][0][:])
+        nc.scalar.copy(h_t[1][:, S // 2:S], hbanks[1][1][:])
         edge_gather(2, 1, "w2dw")
         nc.scalar.copy(h_t[2][:], hbanks[2][:])
         nc.scalar.copy(h_t[3][:], hbanks[3][:])
-        mid = shared.tile([P, 2, HALF], F32, name="rg3mid", offset=2 * S * 4, align_bytes=64)
-        ends = [shared.tile([P, HALF], F32, name="rg3end%d" % a, offset=(2 * S + V) * 4, align_bytes=64) for a in range(2)]
+        mid = shared.tile([P, 2, HALF], F32, name="rg3mid", offset=S * 4 + 128, align_bytes=64)
+        ends = [shared.tile([P, HALF], F32, name="rg3end%d" % a, offset=(S + V) * 4 + 128, align_bytes=64) for a in range(2)]
         rg3 = {(0, 0): ends[0][:], (0, 1): mid[:, 0, :], (1, 0): mid[:, 1, :], (1, 1): ends[1][:]}
 
         def last_edge_gather(a, d):
@@ -211,12 +210,16 @@ def tile_picked_zcomp_sigmoid_po_kernel(tc, x_words, x_scales, e_words, e_scales
                 if a == 0 and d == 0:
                     last_edge_gather(1, 1)
             zb = new("zb%d" % a, [P, HALF, PACK], BF16)
-            nc.vector.tensor_tensor(zb[:].rearrange("p (c i) t -> p c t i", i=2),
-                                    prod[0][:, :, v0:v0 + HALF].rearrange("p t (c i) -> p c t i", i=2),
-                                    prod[1][:, :, v0:v0 + HALF].rearrange("p t (c i) -> p c t i", i=2), ALU.add)
+            n = HALF // (1 + a)
+            for c in range(0, HALF, n):
+                nc.vector.tensor_tensor(zb[:, c:c + n, :].rearrange("p (c i) t -> p c t i", i=2),
+                                        prod[0][:, :, v0 + c:v0 + c + n].rearrange("p t (c i) -> p c t i", i=2),
+                                        prod[1][:, :, v0 + c:v0 + c + n].rearrange("p t (c i) -> p c t i", i=2), ALU.add)
             zw = new("zw%d" % a, [P, HALF], U32)
             zs = new("zs%d" % a, [P, HALF], U8)
-            nc.vector.quantize_mx(out=zw[:].bitcast(FP8X4), scales=zs[:], in_=zb[:].rearrange("p v t -> p (v t)"))
+            for c in range(0, HALF, n):
+                nc.vector.quantize_mx(out=zw[:, c:c + n].bitcast(FP8X4), scales=zs[:, c:c + n],
+                                      in_=zb[:, c:c + n, :].rearrange("p v t -> p (v t)"))
             zq.append((zw, zs))
         for a in range(2):
             v0 = a * HALF

from contextlib import ExitStack

import concourse.mybir as mybir

K, T, S, V, H, N, W = 512, 1024, 512, 256, 512, 512, 1024
FLOPS = 2 * K * H * S * 2 + 2 * H * N * V

F32 = mybir.dt.float32
BF16 = mybir.dt.bfloat16
I32 = mybir.dt.int32
U32 = mybir.dt.uint32
U16 = mybir.dt.uint16
U8 = mybir.dt.uint8
FP8X4 = mybir.dt.float8_e4m3fn_x4
ACT = mybir.ActivationFunctionType
ALU = mybir.AluOpType

P = 128
PACK = 4
HALF = V // 2
W1_CUTS = (0, 128, 384, 512)


def tile_picked_zcomp_sigmoid_po_kernel(tc, x_words, x_scales, e_words, e_scales, w1, w2_words, w2_scales, w3_words, w3_scales,
        offs, pos1, pos2, attr, edge1, edge2, out_0, out_1, out_2):
    nc = tc.nc
    with ExitStack() as ctx:
        sb = ctx.enter_context(tc.tile_pool(name="sb", bufs=1))
        shared = ctx.enter_context(tc.tile_pool(name="shared", bufs=1))
        ps = ctx.enter_context(tc.psum_pool(name="ps", bufs=1))

        def new(name, shape, dtype, tag=None):
            return sb.tile(shape, dtype, name=name, tag=tag or name, align_bytes=64)

        def load_list(name, src):
            t = new(name, list(src.shape), U16)
            nc.sync.dma_start(t[:], src)
            return t

        def load_words(name, src):
            t = new(name, [P, src.shape[2]], U32)
            nc.sync.dma_start(t[:].bitcast(I32), src[0].rearrange("p n t -> p (n t)").bitcast(I32))
            return t

        def load_scales(name, src):
            cols = src.shape[2]
            t = new(name, [P, cols], U8)
            rows = src[0].bitcast(I32)
            for q in range(4):
                nc.sync.dma_start(t[32 * q:32 * q + 32, :].bitcast(I32),
                                  rows[4 * q:4 * q + 4, :].unsqueeze(0).broadcast_to([8, 4, cols // 4]))
            return t

        warm = new("warm", [P, 1], F32)
        warm2 = new("warm2", [P, 1], F32)
        nc.vector.memset(warm[:], 0.0)
        nc.scalar.activation(warm2[:], warm[:], ACT.Sigmoid)

        xs = new("xs", [P, T], U8)
        w2s = new("w2s", [P, H], U8)
        for t in (w2s, xs):
            nc.vector.memset(t[:].bitcast(I32), 0)

        def load_scale_rows(t, src, rows=range(4)):
            for r in rows:
                nc.sync.dma_start(t[r:P:32, :].bitcast(I32), src[0].bitcast(I32)[r:16:4, :])

        w1rows = w1.rearrange("(p j) c -> p j c", j=PACK)

        def load_w1(u):
            c0, c1 = W1_CUTS[u], W1_CUTS[u + 1]
            t = new("w1raw%d" % u, [P, PACK, c1 - c0], F32)
            nc.sync.dma_start(t[:], w1rows[:, :, c0:c1])
            return t

        attr_t = load_list("attr_t", attr)
        es = load_scales("es", e_scales)
        load_scale_rows(w2s, w2_scales, range(1))
        ew = load_words("ew", e_words)
        w2w = load_words("w2w", w2_words)
        load_scale_rows(w2s, w2_scales, range(1, 4))
        nc.sync.dma_start(w2s[4:P:8, :].bitcast(I32), w3_scales[0].bitcast(I32))
        offs_t = load_list("offs_t", offs)
        xw = load_words("xw", x_words)
        w1raw = [load_w1(0)]
        load_scale_rows(xs, x_scales)
        edges = [load_list("edge1_t", edge1)]
        w1raw.append(load_w1(1))
        w1raw.append(load_w1(2))
        w3w = load_words("w3w", w3_words)
        poss = [load_list("pos1_t", pos1), load_list("pos2_t", pos2)]
        edges.append(load_list("edge2_t", edge2))

        def deal(name, src, dtype, tag=None):
            dst = new(name, [P, 512], dtype, tag)
            a, b = (dst[:], src[:]) if dtype == U8 else (dst[:].bitcast(I32), src[:].bitcast(I32))
            nc.vector.tensor_copy(a.rearrange("p (t m) -> p m t", t=PACK), b.rearrange("p (m t) -> p m t", t=PACK))
            return dst

        egw = new("egw", [P, S], U32)
        egs = new("egs", [P, S], U8)
        xgw = new("xgw", [P, S], U32)
        xgs = new("xgs", [P, S], U8)
        nc.vector.tensor_copy(egs[:], es[:].indirect(attr_t[:]))
        nc.vector.tensor_copy(egw[:], ew[:].indirect(attr_t[:]))
        w2dw = deal("w2dw", w2w, U32)
        w2ds = new("w2ds", [P, H], U8)
        for t0, t1 in ((0, 1), (1, PACK)):
            nc.vector.tensor_copy(w2ds[:].rearrange("p (t m) -> p m t", t=PACK)[:, :, t0:t1],
                                  w2s[:].rearrange("p (m t) -> p m t", t=PACK)[:, :, t0:t1])

        w1b = new("w1b", [P, PACK, P, PACK], BF16)

        def round_w1(u, t0=0, t1=PACK):
            nc.vector.tensor_copy(w1b[:, t0:t1, W1_CUTS[u] // PACK:W1_CUTS[u + 1] // PACK, :].rearrange("p t m j -> p m j t"),
                 w1raw[u][:].rearrange("p j (m t) -> p m j t", t=PACK)[:, :, :, t0:t1])

        nc.vector.tensor_copy(xgw[:], xw[:].indirect(offs_t[:]))
        nc.vector.tensor_copy(xgs[:], xs[:].indirect(offs_t[:]))
        round_w1(0)
        round_w1(1)
        round_w1(2, 0, 2)
        round_w1(2, 2, PACK)

        r_t = []
        rg = {}

        def edge_gather(t, d, tag=None):
            rg[t, d] = new("rg%d_%d" % (t, d), [P, V], F32, tag)
            nc.scalar.activation(rg[t, d][:], r_t[t][:].indirect(edges[d][:]), ACT.Sigmoid)

        rbanks = []
        for t in range(PACK):
            bank = ps.tile([P, S], F32, name="rbank%d" % t, tag="r%d" % t)
            cols = slice(t * P, (t + 1) * P)
            nc.tensor.matmul_mx(out=bank[:], lhsT=w2dw[:, cols].bitcast(FP8X4), lhsT_scale=w2ds[:, cols],
                                rhs=egw[:].bitcast(FP8X4), rhs_scale=egs[:], start=True, stop=True)
            rbanks.append(bank)
        for t in range(PACK):
            r_t.append(shared.tile([P, S], F32, name="r1", offset=S * 4, align_bytes=64) if t == 1 else new("r%d" % t, [P, S], F32))
            nc.scalar.copy(r_t[t][:], rbanks[t][:])
        for t in range(PACK - 1):
            edge_gather(t, 0)
        for t in range(2):
            edge_gather(t, 1)

        hbanks = []
        w13s = new("w13s", [P, H], U8)

        def h_product(bank, w1w, t, t0, j0, j1):
            nc.tensor.matmul_mx(out=bank[:], lhsT=w1w[:, (t - t0) * P:(t - t0 + 1) * P].bitcast(FP8X4), lhsT_scale=w13s[:, t * P:(t + 1) * P],
                                rhs=xgw[:, j0:j1].bitcast(FP8X4), rhs_scale=xgs[:, j0:j1], start=True, stop=True)

        for t0, t1 in ((0, 1), (1, 2), (2, PACK)):
            w1w = new("w1w%d" % t0, [P, (t1 - t0) * P], U32, "w2dw" if t0 == 1 else None)
            nc.vector.quantize_mx(out=w1w[:].bitcast(FP8X4), scales=w13s[:, P * t0:P * t1],
                                  in_=w1b[:, t0:t1, :, :].rearrange("p t m j -> p (t m j)"))
            for t in range(t0, t1):
                if t > 1:
                    hbanks.append(ps.tile([P, S], F32, name="hbank%d" % t, tag="h%d" % t))
                    h_product(hbanks[t], w1w, t, t0, 0, S)
                else:
                    hbanks.append([ps.tile([P, S // 2], F32, name="hbank%d_%d" % (t, a), tag="%s%d" % ("hr"[a], t)) for a in range(2)])
                    for a in range(2):
                        h_product(hbanks[t][a], w1w, t, t0, a * S // 2, (a + 1) * S // 2)

        for r in range(4):
            nc.sync.dma_start(w13s[4 + r:P:32, :].bitcast(I32), w2ds[8 * r + 4:P:32, :].bitcast(I32))
        w3dw = deal("w3dw", w3w, U32)
        h_t = [new("h0", [P, S], F32), new("h1", [P, S], F32, "r0"),
               shared.tile([P, S], F32, name="h2", offset=64, align_bytes=64), new("h3", [P, S], F32, "r2")]
        for a in range(2):
            nc.vector.tensor_copy(h_t[0][:, a * S // 2:(a + 1) * S // 2], hbanks[0][a][:])
        nc.vector.tensor_copy(h_t[1][:, 0:S // 2], hbanks[1][0][:])
        nc.scalar.copy(h_t[1][:, S // 2:S], hbanks[1][1][:])
        edge_gather(2, 1, "w2dw")
        nc.scalar.copy(h_t[2][:], hbanks[2][:])
        nc.scalar.copy(h_t[3][:], hbanks[3][:])
        mid = shared.tile([P, 2, HALF], F32, name="rg3mid", offset=S * 4 + 128, align_bytes=64)
        ends = [shared.tile([P, HALF], F32, name="rg3end%d" % a, offset=(S + V) * 4 + 128, align_bytes=64) for a in range(2)]
        rg3 = {(0, 0): ends[0][:], (0, 1): mid[:, 0, :], (1, 0): mid[:, 1, :], (1, 1): ends[1][:]}

        def last_edge_gather(a, d):
            nc.scalar.activation(rg3[a, d], r_t[3][:].indirect(edges[d][:, a * HALF // 16:(a + 1) * HALF // 16]), ACT.Sigmoid)

        last_edge_gather(0, 0)
        last_edge_gather(0, 1)
        last_edge_gather(1, 0)

        prod = [new("prod%d" % d, [P, PACK, V], F32) for d in range(2)]

        def node_gathers(t, v0, n):
            for d in range(2):
                nc.vector.tensor_tensor(prod[d][:, t, v0:v0 + n], h_t[t][:].indirect(poss[d][:, v0 // 16:(v0 + n) // 16]),
                                        rg[t, d][:, v0:v0 + n], ALU.mult)

        for t in range(PACK - 1):
            node_gathers(t, 0, V)

        ys = new("ys", [P, V], U8)
        yw = new("yw", [P, V], U32)
        out_rows = out_0.rearrange("(p t) v -> p t v", t=PACK)
        out_words = out_1[0].rearrange("p n t -> p (n t)").bitcast(I32)
        zq = []
        for a in range(2):
            v0 = a * HALF
            for d in range(2):
                nc.vector.tensor_tensor(prod[d][:, 3, v0:v0 + HALF], h_t[3][:].indirect(poss[d][:, v0 // 16:(v0 + HALF) // 16]),
                                        rg3[a, d], ALU.mult)
                if a == 0 and d == 0:
                    last_edge_gather(1, 1)
            zb = new("zb%d" % a, [P, HALF, PACK], BF16)
            n = HALF // (1 + a)
            for c in range(0, HALF, n):
                nc.vector.tensor_tensor(zb[:, c:c + n, :].rearrange("p (c i) t -> p c t i", i=2),
                                        prod[0][:, :, v0 + c:v0 + c + n].rearrange("p t (c i) -> p c t i", i=2),
                                        prod[1][:, :, v0 + c:v0 + c + n].rearrange("p t (c i) -> p c t i", i=2), ALU.add)
            zw = new("zw%d" % a, [P, HALF], U32)
            zs = new("zs%d" % a, [P, HALF], U8)
            for c in range(0, HALF, n):
                nc.vector.quantize_mx(out=zw[:, c:c + n].bitcast(FP8X4), scales=zs[:, c:c + n],
                                      in_=zb[:, c:c + n, :].rearrange("p v t -> p (v t)"))
            zq.append((zw, zs))
        for a in range(2):
            v0 = a * HALF
            zw, zs = zq[a]
            yb = new("yb%d" % a, [P, HALF, PACK], BF16)
            y = new("y%d" % a, [P, PACK, HALF], F32)
            nb = 1 + a
            per = PACK // nb
            banks = [ps.tile([P, per, HALF], F32, name="ybank%d_%d" % (a, k), tag="r%d" % (a + k)) for k in range(nb)]
            for t in range(PACK):
                cols = slice(t * P, (t + 1) * P)
                nc.tensor.matmul_mx(out=banks[t // per][:, t % per, :], lhsT=w3dw[:, cols].bitcast(FP8X4), lhsT_scale=w13s[4:P, cols],
                                    rhs=zw[:].bitcast(FP8X4), rhs_scale=zs[:], start=True, stop=True)
            if a == 0:
                nc.scalar.copy(y[:], banks[0][:])
                nc.sync.dma_start(out_rows[:, :, v0:v0 + HALF], y[:])
                nc.scalar.copy(yb[:].rearrange("p (c i) t -> p c t i", i=2),
                               banks[0][:].rearrange("p t (c i) -> p c t i", i=2))
            else:
                for k in range(nb):
                    rows = slice(k * per, (k + 1) * per)
                    nc.vector.tensor_copy(yb[:, :, rows].rearrange("p (c i) t -> p c t i", i=2),
                                          banks[k][:].rearrange("p t (c i) -> p c t i", i=2))
                    nc.scalar.copy(y[:, rows, :], banks[k][:])
                    (nc.scalar if k else nc.sync).dma_start(out_rows[:, rows, v0:v0 + HALF], y[:, rows, :])
            nc.vector.quantize_mx(out=yw[:, v0:v0 + HALF].bitcast(FP8X4), scales=ys[:, v0:v0 + HALF], in_=yb[:].rearrange("p v t -> p (v t)"))
        nc.sync.dma_start(out_words, yw[:].bitcast(I32))
        for r in range(4):
            eng = nc.sync if r < 2 else nc.scalar
            eng.dma_start(out_2[0].bitcast(I32)[r:16:4, :], ys[r:P:32, :].bitcast(I32))
